import numpy as np
import ml_dtypes


def mxq(x, axis, fmt="e4m3"):
    dtype, down = {"e4m3": (ml_dtypes.float8_e4m3fn, 7), "e5m2": (ml_dtypes.float8_e5m2, 14)}[fmt]
    v = np.moveaxis(np.asarray(x, np.float32).astype(ml_dtypes.bfloat16).astype(np.float64), axis, -1)
    blocks = v.reshape(v.shape[:-1] + (-1, 32))
    amax = np.abs(blocks).max(-1, keepdims=True)
    byte = np.maximum(np.where(amax > 0, np.frexp(amax)[1] - 1 + 127, 0) - down, 1)
    scale = np.exp2(byte - 127.0)
    codes = (blocks / scale).astype(np.float32).astype(dtype).astype(np.float64)
    return np.moveaxis((codes * scale).reshape(v.shape), -1, axis)


WIDE = False


def mx_kscale(k):
    if not WIDE:
        return np.ones(k)
    levels = np.array([10, -10, 5, -5, 0])
    if k % 512:
        return np.exp2(np.random.permutation(np.resize(levels, k // 32))).repeat(32)
    a = np.empty((k // 512, 16))
    for p in range(k // 512):
        a[p, :8] = np.random.permutation(np.resize(levels, 8))
        for g in range(8):
            far = levels[np.abs(levels - a[p, g]) >= 10]
            a[p, g + 8] = far[np.random.randint(len(far))]
    return np.exp2(a.ravel()).repeat(32)


BF16 = ml_dtypes.bfloat16


def bf(x):
    return np.asarray(x, np.float32).astype(BF16)


def f64(x):
    return np.asarray(x).astype(np.float64)


N, P, C, D = 2048, 1024, 512, 512


def gelu(z):
    return 0.5 * z * (1.0 + np.tanh(np.sqrt(2.0 / np.pi) * (z + 0.044715 * z ** 3)))


def setup_inputs():
    s, t, r = mx_kscale(C), mx_kscale(P), mx_kscale(C)
    angle = 2.0 * np.pi * np.random.random((N, 1)) * np.arange(1, P + 1)
    return {"x_re": bf(np.random.standard_normal((P, C)) * s * t[:, None]),
            "x_im": bf(np.random.standard_normal((P, C)) * s * t[:, None]),
            "r_re": bf(np.random.standard_normal((C, D)) / np.sqrt(2.0 * C) / s[:, None]),
            "r_im": bf(np.random.standard_normal((C, D)) / np.sqrt(2.0 * C) / s[:, None]),
            "g_re": bf(1.0 + 0.3 * np.random.standard_normal((P, D))),
            "g_im": bf(0.3 * np.random.standard_normal((P, D))),
            "basis_cos": bf(np.cos(angle) / np.sqrt(P) / t),
            "basis_sin": bf(np.sin(angle) / np.sqrt(P) / t),
            "u": bf(np.random.standard_normal((N, C)) * r),
            "w": bf(np.random.standard_normal((C, D)) / np.sqrt(C) / r[:, None]),
            "bias": bf(0.3 * np.random.standard_normal(D))}


def reference(x_re, x_im, r_re, r_im, g_re, g_im, basis_cos, basis_sin, u, w, bias):
    xr, xi = mxq(f64(x_re), 1, "e4m3"), mxq(f64(x_im), 1, "e4m3")
    rr, ri = mxq(f64(r_re), 0, "e4m3"), mxq(f64(r_im), 0, "e4m3")
    y_re = (xr @ rr) - (xi @ ri)
    y_im = (xr @ ri) + (xi @ rr)
    gr, gi = f64(g_re), f64(g_im)
    z_re = gr * y_re - gi * y_im
    z_im = gr * y_im + gi * y_re
    field = ((mxq(f64(basis_cos), 1, "e4m3") @ mxq(z_re, 0, "e4m3"))
             - (mxq(f64(basis_sin), 1, "e4m3") @ mxq(z_im, 0, "e4m3")))
    skip = mxq(f64(u), 1, "e4m3") @ mxq(f64(w), 0, "e4m3")
    return gelu(field + skip + f64(bias))

@@ -1,0 +1,337 @@
+from contextlib import ExitStack
+
+import concourse.mybir as mybir
+from concourse.masks import make_identity
+
+N, P, C, D = 2048, 1024, 512, 512
+
+FLOPS = 2 * (4 * P * C * D + 2 * N * P * D + N * C * D)
+
+F32 = mybir.dt.float32
+BF16 = mybir.dt.bfloat16
+U32 = mybir.dt.uint32
+U8 = mybir.dt.uint8
+FP8X4 = mybir.dt.float8_e4m3fn_x4
+ALU = mybir.AluOpType
+ACT = mybir.ActivationFunctionType
+
+LANES = 128
+RAW_BUFS = 22
+
+
+def tile_fourier_operator_mix_f4_kernel(
+    tc, x_re, x_im, r_re, r_im, g_re, g_im, basis_cos, basis_sin, u, w, bias, out
+):
+    nc = tc.nc
+    with ExitStack() as ctx:
+        ctx.enter_context(tc.manual_schedule())
+        raw_pool = ctx.enter_context(tc.tile_pool(name="raw", bufs=RAW_BUFS))
+        keep = ctx.enter_context(tc.tile_pool(name="keep", bufs=1))
+        grp_pool = ctx.enter_context(tc.tile_pool(name="grp", bufs=4))
+        zgrp_pool = ctx.enter_context(tc.tile_pool(name="zgrp", bufs=2))
+        basis_pool = ctx.enter_context(tc.tile_pool(name="basis", bufs=12))
+        prod_pool = ctx.enter_context(tc.tile_pool(name="prod", bufs=2))
+        out_pool = ctx.enter_context(tc.tile_pool(name="outs", bufs=2))
+        psum = ctx.enter_context(tc.psum_pool(name="psum", bufs=4))
+
+        xv = {
+            "re": x_re.rearrange("(g m t) k -> g m t k", g=2, t=4),
+            "im": x_im.rearrange("(g m t) k -> g m t k", g=2, t=4),
+        }
+        gv = {
+            "re": g_re.rearrange("(g m t) d -> g m t d", g=2, t=4),
+            "im": g_im.rearrange("(g m t) d -> g m t d", g=2, t=4),
+        }
+        bv = {
+            "cos": basis_cos.rearrange("(q p j) k -> q p j k", q=4, j=4),
+            "sin": basis_sin.rearrange("(q p j) k -> q p j k", q=4, j=4),
+        }
+        uv = u.rearrange("(q p j) k -> q p j k", q=4, j=4)
+        ov = out.rearrange("(q p j) d -> q p j d", q=4, j=4)
+
+        def weights_view(t):
+            return t.rearrange("(p j) d -> p j d", j=4)
+
+        sources = [
+            ("x", "re", 0), ("r", "re"), ("x", "im", 0), ("r", "im"),
+            ("cos", 0, 0), ("sin", 0, 0),
+            ("g", "re", 0), ("g", "im", 0),
+            ("x", "re", 1), ("x", "im", 1),
+            ("u", 0), ("cos", 0, 1), ("sin", 0, 1),
+            ("g", "re", 1), ("g", "im", 1), ("w",),
+        ]
+        for q in range(1, 4):
+            sources += [("cos", q, 0), ("sin", q, 0), ("u", q), ("cos", q, 1), ("sin", q, 1)]
+        raws = {}
+
+        def load(count):
+            for step in range(count):
+                if not sources:
+                    return
+                key = sources[0]
+                sources.remove(key)
+                t = raw_pool.tile([LANES, 2048], BF16, name="raw", tag="raw", align_bytes=64)
+                kind = key[0]
+                if kind == "x":
+                    src = xv[key[1]][key[2]]
+                elif kind == "g":
+                    src = gv[key[1]][key[2]]
+                elif kind == "r":
+                    src = weights_view(r_re if key[1] == "re" else r_im)
+                elif kind == "w":
+                    src = weights_view(w)
+                elif kind == "u":
+                    src = uv[key[1]]
+                else:
+                    src = bv[kind][key[1]][:, 2 * key[2] : 2 * key[2] + 2, :]
+                nc.sync.dma_start(
+                    out=t[:].rearrange("p (a b) -> p a b", a=src.shape[1]), in_=src
+                )
+                raws[key] = t
+
+        load(RAW_BUFS)
+
+        ident = keep.tile([LANES, LANES], F32, name="ident")
+        make_identity(nc, ident[:])
+        dummy = keep.tile([LANES, 1], F32, name="dummy")
+        nc.vector.memset(dummy[:], 0.0)
+        warm = keep.tile([LANES, 1], F32, name="warm")
+        nc.scalar.activation(out=warm[:], in_=dummy[:], func=ACT.Gelu_apprx_tanh)
+        ones = keep.tile([LANES, LANES], BF16, name="ones")
+        nc.vector.memset(ones[:], 1.0)
+        bias_row = keep.tile([LANES, D], BF16, name="bias_row")
+        nc.vector.memset(bias_row[:], 0.0)
+        nc.scalar.dma_start(out=bias_row[0:1, :], in_=bias.unsqueeze(0))
+        bias_sb = keep.tile([LANES, D], F32, name="bias_sb")
+
+        x_codes = keep.tile([LANES, 4 * 512], U32, name="x_codes", align_bytes=64)
+        x_scales = keep.tile([LANES, 4 * 512], U8, name="x_scales", align_bytes=64)
+        r_codes = keep.tile([LANES, 3 * 512], U32, name="r_codes", align_bytes=64)
+        r_scales = keep.tile([LANES, 3 * 512], U8, name="r_scales", align_bytes=64)
+        w_codes = keep.tile([LANES, 512], U32, name="w_codes", align_bytes=64)
+        w_scales = keep.tile([LANES, 512], U8, name="w_scales", align_bytes=64)
+        z_codes = keep.tile([LANES, 4 * 512], U32, name="z_codes", align_bytes=64)
+        z_scales = keep.tile([LANES, 4 * 512], U8, name="z_scales", align_bytes=64)
+        u_codes = keep.tile([LANES, 4 * 512], U32, name="u_codes", align_bytes=64)
+        u_scales = keep.tile([LANES, 4 * 512], U8, name="u_scales", align_bytes=64)
+        basis_codes = {}
+
+        def quantize(codes, scales, grouped):
+            nc.vector.quantize_mx(out=codes.bitcast(FP8X4), scales=scales, in_=grouped)
+
+        def mx(acc, lhs, lhs_cols, rhs, rhs_cols, start, stop):
+            nc.tensor.matmul_mx(
+                out=acc,
+                lhsT=lhs[0][:, lhs_cols].bitcast(FP8X4),
+                lhsT_scale=lhs[1][:, lhs_cols],
+                rhs=rhs[0][:, rhs_cols].bitcast(FP8X4),
+                rhs_scale=rhs[1][:, rhs_cols],
+                start=start,
+                stop=stop,
+            )
+
+        def job_blocks(job):
+            kind = job[0]
+            if kind == "x":
+                t = raws[("x", job[1], job[2])]
+                return [(t, 256 * s) for s in range(4)]
+            if kind == "u":
+                t = raws[("u", job[1])]
+                return [(t, 256 * s) for s in range(4)]
+            q, j = job[1] // 4, job[1] % 4
+            blocks = []
+            for name in ("cos", "sin"):
+                t = raws[(name, q, j // 2)]
+                blocks += [(t, 512 * (j % 2) + 256 * g) for g in range(2)]
+            return blocks
+
+        def job_target(job):
+            kind = job[0]
+            if kind == "x":
+                s = (2 if job[1] == "im" else 0) + job[2]
+                return x_codes[:, 512 * s : 512 * s + 512], x_scales[:, 512 * s : 512 * s + 512]
+            if kind == "u":
+                s = job[1]
+                return u_codes[:, 512 * s : 512 * s + 512], u_scales[:, 512 * s : 512 * s + 512]
+            codes = basis_pool.tile([LANES, 512], U32, name="b_codes", tag="b_codes", align_bytes=64)
+            scales = basis_pool.tile([LANES, 512], U8, name="b_scales", tag="b_scales", align_bytes=64)
+            basis_codes[job[1]] = (codes, scales)
+            return codes[:], scales[:]
+
+        jobs = [("x", "re", 0), ("x", "im", 0), ("b", 0), ("b", 1), ("x", "re", 1), ("x", "im", 1), ("u", 0), ("b", 2), ("b", 3)]
+        for q in range(1, 4):
+            jobs += [("b", 4 * q), ("b", 4 * q + 1), ("u", q), ("b", 4 * q + 2), ("b", 4 * q + 3)]
+        units = [(job, half) for job in jobs for half in range(2)]
+        groups = {}
+        ready = []
+
+        def transpose_units(count):
+            taken = units[:count]
+            for unit in taken:
+                units.remove(unit)
+                job, half = unit
+                if half == 0:
+                    groups[job] = grp_pool.tile([LANES, 2048], BF16, name="grp", tag="grp", align_bytes=64)
+                tp = psum.tile([LANES, 512], F32, name="tp", tag="tp")
+                blocks = job_blocks(job)[2 * half : 2 * half + 2]
+                for a, (t, base) in enumerate(blocks):
+                    words = t[:].bitcast(F32)
+                    for v in range(2):
+                        nc.tensor.transpose(
+                            tp[:, 256 * a + 128 * v : 256 * a + 128 * v + 128],
+                            words[:, base + v : base + 256 : 2],
+                            ident[:],
+                        )
+                gw = groups[job][:].bitcast(F32)[:, 512 * half : 512 * half + 512]
+                nc.scalar.copy(
+                    out=gw.rearrange("p (a r v) -> p a r v", a=2, v=2),
+                    in_=tp[:].rearrange("p (a v r) -> p a r v", a=2, v=2),
+                )
+                if half == 1:
+                    ready.append(job)
+
+        def quantize_ready():
+            for job in list(ready):
+                ready.remove(job)
+                codes, scales = job_target(job)
+                quantize(codes, scales, groups[job][:])
+
+        def interleave(eng_copy, grouped, raw, lo, hi):
+            eng_copy(
+                out=grouped[:].rearrange("p (d j) -> p d j", j=4)[:, lo:hi, :],
+                in_=raw[:].rearrange("p (j d) -> p d j", j=4)[:, lo:hi, :],
+            )
+
+        def grp_tile():
+            return grp_pool.tile([LANES, 2048], BF16, name="grp", tag="wgrp", bufs=2, align_bytes=64)
+
+        R_RE, R_IM, R_NEG = 0, 1, 2
+
+        def r_cols(which, lo=0, width=512):
+            return slice(512 * which + lo, 512 * which + lo + width)
+
+        transpose_units(2)
+        g_rr = grp_tile()
+        interleave(nc.vector.tensor_copy, g_rr, raws[("r", "re")], 0, 512)
+        quantize_ready()
+        quantize(r_codes[:, r_cols(R_RE)], r_scales[:, r_cols(R_RE)], g_rr[:])
+        transpose_units(2)
+        g_ri = grp_tile()
+        interleave(nc.vector.tensor_copy, g_ri, raws[("r", "im")], 0, 352)
+        interleave(nc.scalar.copy, g_ri, raws[("r", "im")], 352, 512)
+        quantize_ready()
+        quantize(r_codes[:, r_cols(R_IM)], r_scales[:, r_cols(R_IM)], g_ri[:])
+        g_rn = grp_tile()
+        nc.vector.tensor_scalar(out=g_rn[:], in0=g_ri[:], scalar1=-1.0, scalar2=None, op0=ALU.mult)
+        transpose_units(4)
+        quantize(r_codes[:, r_cols(R_NEG)], r_scales[:, r_cols(R_NEG)], g_rn[:])
+
+        bias_ps = psum.tile([LANES, 512], F32, name="bias_ps", tag="acc")
+        nc.tensor.matmul(bias_ps[:], lhsT=ones[:], rhs=bias_row[:], start=True, stop=True)
+        nc.scalar.copy(out=bias_sb[:], in_=bias_ps[:])
+
+        xq = (x_codes, x_scales)
+        rq = (r_codes, r_scales)
+        wq = (w_codes, w_scales)
+        zq = (z_codes, z_scales)
+        uq = (u_codes, u_scales)
+
+        z_groups = {}
+        pending_add = []
+        z_ready = []
+
+        def emit_adds():
+            for g, dq, prods in list(pending_add):
+                pending_add.remove((g, dq, prods))
+                a, b, c, e = prods
+                cols = slice(512 * dq, 512 * dq + 512)
+                nc.gpsimd.tensor_tensor(out=z_groups[("re", g)][:, cols], in0=a[:], in1=b[:], op=ALU.subtract)
+                nc.gpsimd.tensor_tensor(out=z_groups[("im", g)][:, cols], in0=c[:], in1=e[:], op=ALU.subtract)
+                if dq == 3:
+                    z_ready.append(g)
+
+        def quantize_z():
+            for g in list(z_ready):
+                z_ready.remove(g)
+                for s, name in enumerate(("re", "im")):
+                    cols = slice(512 * (2 * s + g), 512 * (2 * s + g) + 512)
+                    quantize(z_codes[:, cols], z_scales[:, cols], z_groups[(name, g)][:])
+
+        def stage1(g, dq):
+            if dq == 0:
+                for name in ("re", "im"):
+                    z_groups[(name, g)] = zgrp_pool.tile([LANES, 2048], BF16, name="z_" + name, tag="z_" + name, align_bytes=64)
+            yi = psum.tile([LANES, 512], F32, name="yi", tag="acc")
+            yr = psum.tile([LANES, 512], F32, name="yr", tag="acc")
+            for acc, first, second in ((yi, R_IM, R_RE), (yr, R_RE, R_NEG)):
+                for t in range(4):
+                    o = acc[:, 128 * t : 128 * t + 128]
+                    re_cols = slice(512 * g + 128 * t, 512 * g + 128 * t + 128)
+                    im_cols = slice(1024 + 512 * g + 128 * t, 1024 + 512 * g + 128 * t + 128)
+                    mx(o, xq, re_cols, rq, r_cols(first, 128 * dq, 128), True, False)
+                    mx(o, xq, im_cols, rq, r_cols(second, 128 * dq, 128), False, True)
+            a = prod_pool.tile([LANES, 512], F32, name="pa", tag="pa")
+            b = prod_pool.tile([LANES, 512], F32, name="pb", tag="pb")
+            c = prod_pool.tile([LANES, 512], F32, name="pc", tag="pc")
+            e = prod_pool.tile([LANES, 512], F32, name="pe", tag="pe")
+
+            def spread(t):
+                return t[:].rearrange("p (n t) -> p n t", t=4)
+
+            yiv = yi[:].rearrange("p (t n) -> p n t", t=4)
+            yrv = yr[:].rearrange("p (t n) -> p n t", t=4)
+            gr = raws[("g", "re", g)][:].rearrange("p (t d) -> p d t", t=4)[:, 128 * dq : 128 * dq + 128, :]
+            gi = raws[("g", "im", g)][:].rearrange("p (t d) -> p d t", t=4)[:, 128 * dq : 128 * dq + 128, :]
+            nc.vector.scalar_tensor_tensor(out=spread(c), in0=yiv, scalar=-1.0, in1=gr, op0=ALU.mult, op1=ALU.mult)
+            nc.vector.tensor_tensor(out=spread(b), in0=yiv, in1=gi, op=ALU.mult)
+            nc.vector.tensor_tensor(out=spread(a), in0=yrv, in1=gr, op=ALU.mult)
+            nc.vector.tensor_tensor(out=spread(e), in0=yrv, in1=gi, op=ALU.mult)
+            pending_add.append((g, dq, (a, b, c, e)))
+
+        for i in range(8):
+            stage1(i // 4, i % 4)
+            transpose_units(3)
+            emit_adds()
+            quantize_ready()
+            quantize_z()
+            if i == 0:
+                load(4)
+            elif i == 3:
+                load(4)
+            elif i == 4:
+                load(4)
+            if i == 5:
+                g_w = grp_tile()
+                interleave(nc.scalar.copy, g_w, raws[("w",)], 0, 512)
+            if i == 6:
+                quantize(w_codes[:], w_scales[:], g_w[:])
+
+        pending_gelu = []
+
+        def emit_gelu():
+            for n, v, o in list(pending_gelu):
+                pending_gelu.remove((n, v, o))
+                nc.scalar.activation(out=o[:, 512 * (n % 2) : 512 * (n % 2) + 512], in_=v[:], func=ACT.Gelu_apprx_tanh)
+                if n % 2 == 1:
+                    q, j = n // 4, n % 4
+                    nc.sync.dma_start(out=ov[q][:, j - 1 : j + 1, :], in_=o[:].rearrange("p (a d) -> p a d", a=2))
+
+        for k in range(8):
+            transpose_units(4)
+            accs = []
+            for n in (2 * k, 2 * k + 1):
+                acc = psum.tile([LANES, 512], F32, name="acc", tag="acc")
+                bq = basis_codes[n]
+                mx(acc[:], uq, slice(128 * n, 128 * n + 128), wq, slice(0, 512), True, False)
+                for s in range(2):
+                    for g in range(2):
+                        mx(acc[:], bq, slice(256 * s + 128 * g, 256 * s + 128 * g + 128), zq, slice(1024 * s + 512 * g, 1024 * s + 512 * g + 512), False, s == 1 and g == 1)
+                accs.append((n, acc))
+            quantize_ready()
+            emit_gelu()
+            o = out_pool.tile([LANES, 1024], F32, name="o", tag="o")
+            for n, acc in accs:
+                v = out_pool.tile([LANES, 512], F32, name="v", tag="v")
+                nc.vector.tensor_tensor(out=v[:], in0=acc[:], in1=bias_sb[:], op=ALU.add)
+                pending_gelu.append((n, v, o))
+        emit_gelu()

@@ -16,7 +16,26 @@ ALU = mybir.AluOpType
 ACT = mybir.ActivationFunctionType
 
 LANES = 128
-RAW_BUFS = 22
+CFG = {
+    "raw_bufs": 24,
+    "b_bufs": 8,
+    "t_run": [5,5,5,5,5,5,5,5],
+    "t_pair": [2,2,2,2,2,2,2,2],
+    "q_run": [4,4,1,1,1,1,1,1],
+    "q_first": 1,
+    "g_re": [0,0,0,0,0,0,0,0],
+    "g_im": [0,0,0,0,0,0,0,0],
+    "reorder": {},
+    "re_ahead": 3,
+    "head_t": 4,
+    "w_step": 4,
+    "w_eng": "S",
+    "ri_split": 256,
+    "bias_g": [0,0,0,0,0,0,0,0,0,0,0,0,0,0,0,0],
+    "r1_re": "S",
+    "r1_im": "S",
+    "neg_eng": ["V","V"],
+}
 
 
 def tile_fourier_operator_mix_f4_kernel(
@@ -25,13 +44,14 @@ def tile_fourier_operator_mix_f4_kernel(
     nc = tc.nc
     with ExitStack() as ctx:
         ctx.enter_context(tc.manual_schedule())
-        raw_pool = ctx.enter_context(tc.tile_pool(name="raw", bufs=RAW_BUFS))
+        raw_pool = ctx.enter_context(tc.tile_pool(name="raw", bufs=CFG["raw_bufs"]))
         keep = ctx.enter_context(tc.tile_pool(name="keep", bufs=1))
-        grp_pool = ctx.enter_context(tc.tile_pool(name="grp", bufs=4))
-        zgrp_pool = ctx.enter_context(tc.tile_pool(name="zgrp", bufs=2))
-        basis_pool = ctx.enter_context(tc.tile_pool(name="basis", bufs=12))
+        wgrp_pool = ctx.enter_context(tc.tile_pool(name="wgrp", bufs=3))
+        zgrp_pool = ctx.enter_context(tc.tile_pool(name="zgrp", bufs=1))
+        basis_pool = ctx.enter_context(tc.tile_pool(name="basis", bufs=CFG["b_bufs"]))
         prod_pool = ctx.enter_context(tc.tile_pool(name="prod", bufs=2))
         out_pool = ctx.enter_context(tc.tile_pool(name="outs", bufs=2))
+        re_pool = ctx.enter_context(tc.tile_pool(name="reord", bufs=5))
         psum = ctx.enter_context(tc.psum_pool(name="psum", bufs=4))
 
         xv = {
@@ -48,16 +68,14 @@ def tile_fourier_operator_mix_f4_kernel(
         }
         uv = u.rearrange("(q p j) k -> q p j k", q=4, j=4)
         ov = out.rearrange("(q p j) d -> q p j d", q=4, j=4)
-
-        def weights_view(t):
-            return t.rearrange("(p j) d -> p j d", j=4)
+        rv = {"re": r_re.rearrange("(p j) d -> p j d", j=4), "im": r_im.rearrange("(p j) d -> p j d", j=4)}
+        wv = w.rearrange("(p j) d -> p j d", j=4)
 
         sources = [
-            ("x", "re", 0), ("r", "re"), ("x", "im", 0), ("r", "im"),
-            ("cos", 0, 0), ("sin", 0, 0),
-            ("g", "re", 0), ("g", "im", 0),
-            ("x", "re", 1), ("x", "im", 1),
-            ("u", 0), ("cos", 0, 1), ("sin", 0, 1),
+            ("x", "re", 0, 0), ("x", "re", 0, 1), ("r", "re", 0), ("x", "im", 0, 0), ("x", "im", 0, 1), ("r", "im", 0),
+            ("g", "re", 0), ("g", "im", 0), ("r", "re", 1), ("r", "im", 1),
+            ("x", "re", 1, 0), ("x", "re", 1, 1), ("x", "im", 1, 0), ("x", "im", 1, 1),
+            ("cos", 0, 0), ("sin", 0, 0), ("u", 0), ("cos", 0, 1), ("sin", 0, 1),
             ("g", "re", 1), ("g", "im", 1), ("w",),
         ]
         for q in range(1, 4):
@@ -70,26 +88,30 @@ def tile_fourier_operator_mix_f4_kernel(
                     return
                 key = sources[0]
                 sources.remove(key)
-                t = raw_pool.tile([LANES, 2048], BF16, name="raw", tag="raw", align_bytes=64)
                 kind = key[0]
+                part = None
+                base = key
                 if kind == "x":
-                    src = xv[key[1]][key[2]]
+                    base, part = key[:3], key[3]
+                    src = xv[key[1]][key[2]][:, 2 * part : 2 * part + 2, :]
                 elif kind == "g":
                     src = gv[key[1]][key[2]]
                 elif kind == "r":
-                    src = weights_view(r_re if key[1] == "re" else r_im)
+                    base, part = key[:2], key[2]
+                    src = rv[key[1]][:, :, 256 * part : 256 * part + 256]
                 elif kind == "w":
-                    src = weights_view(w)
+                    src = wv
                 elif kind == "u":
                     src = uv[key[1]]
                 else:
                     src = bv[kind][key[1]][:, 2 * key[2] : 2 * key[2] + 2, :]
-                nc.sync.dma_start(
-                    out=t[:].rearrange("p (a b) -> p a b", a=src.shape[1]), in_=src
-                )
-                raws[key] = t
+                if base not in raws:
+                    raws[base] = raw_pool.tile([LANES, 2048], BF16, name="raw", tag="raw", align_bytes=64)
+                t = raws[base]
+                dst = t[:] if part is None else t[:, 1024 * part : 1024 * part + 1024]
+                nc.sync.dma_start(out=dst.rearrange("p (a b) -> p a b", a=src.shape[1]), in_=src)
 
-        load(RAW_BUFS)
+        load(22 + CFG["raw_bufs"] - 16)
 
         ident = keep.tile([LANES, LANES], F32, name="ident")
         make_identity(nc, ident[:])
@@ -130,105 +152,121 @@ def tile_fourier_operator_mix_f4_kernel(
                 stop=stop,
             )
 
-        def job_blocks(job):
-            kind = job[0]
-            if kind == "x":
-                t = raws[("x", job[1], job[2])]
-                return [(t, 256 * s) for s in range(4)]
-            if kind == "u":
-                t = raws[("u", job[1])]
-                return [(t, 256 * s) for s in range(4)]
-            q, j = job[1] // 4, job[1] % 4
-            blocks = []
-            for name in ("cos", "sin"):
-                t = raws[(name, q, j // 2)]
-                blocks += [(t, 512 * (j % 2) + 256 * g) for g in range(2)]
-            return blocks
-
-        def job_target(job):
-            kind = job[0]
-            if kind == "x":
-                s = (2 if job[1] == "im" else 0) + job[2]
-                return x_codes[:, 512 * s : 512 * s + 512], x_scales[:, 512 * s : 512 * s + 512]
-            if kind == "u":
-                s = job[1]
-                return u_codes[:, 512 * s : 512 * s + 512], u_scales[:, 512 * s : 512 * s + 512]
-            codes = basis_pool.tile([LANES, 512], U32, name="b_codes", tag="b_codes", align_bytes=64)
-            scales = basis_pool.tile([LANES, 512], U8, name="b_scales", tag="b_scales", align_bytes=64)
-            basis_codes[job[1]] = (codes, scales)
-            return codes[:], scales[:]
-
-        jobs = [("x", "re", 0), ("x", "im", 0), ("b", 0), ("b", 1), ("x", "re", 1), ("x", "im", 1), ("u", 0), ("b", 2), ("b", 3)]
+        units = []
+        for part in range(2):
+            units.append(("x", "re", 0, part))
+        for part in range(2):
+            units.append(("x", "im", 0, part))
+        units += [("x", name, 1, part) for name in ("re", "im") for part in range(2)]
+        units += [("cos", 0), ("sin", 0), ("cos", 1), ("sin", 1)]
+        units += [("u", 0, 0), ("u", 0, 1), ("cos", 2), ("sin", 2), ("cos", 3), ("sin", 3)]
         for q in range(1, 4):
-            jobs += [("b", 4 * q), ("b", 4 * q + 1), ("u", q), ("b", 4 * q + 2), ("b", 4 * q + 3)]
-        units = [(job, half) for job in jobs for half in range(2)]
-        groups = {}
-        ready = []
+            for j in range(4):
+                if j == 2:
+                    units += [("u", q, 0), ("u", q, 1)]
+                units += [("cos", 4 * q + j), ("sin", 4 * q + j)]
+        order = {unit: i for i, unit in enumerate(units)}
+        to_quant = []
+        reordered = {}
+
+        def place(unit):
+            kind = unit[0]
+            if kind == "x":
+                return raws[unit[:3]], unit[3]
+            if kind == "u":
+                return raws[unit[:2]], unit[2]
+            n = unit[1]
+            return raws[(kind, n // 4, (n % 4) // 2)], n % 2
+
+        def target(unit):
+            kind = unit[0]
+            if kind == "x":
+                c = 1024 * (unit[1] == "im") + 512 * unit[2] + 256 * unit[3]
+                return x_codes[:, c : c + 256], x_scales[:, c : c + 256]
+            if kind == "u":
+                c = 512 * unit[1] + 256 * unit[2]
+                return u_codes[:, c : c + 256], u_scales[:, c : c + 256]
+            n = unit[1]
+            if n not in basis_codes:
+                codes = basis_pool.tile([LANES, 512], U32, name="b_codes", tag="b_codes", align_bytes=64)
+                scales = basis_pool.tile([LANES, 512], U8, name="b_scales", tag="b_scales", align_bytes=64)
+                basis_codes[n] = (codes, scales)
+            codes, scales = basis_codes[n]
+            c = 256 * (kind == "sin")
+            return codes[:, c : c + 256], scales[:, c : c + 256]
+
+        def reorder(count):
+            for unit in units[:count]:
+                eng = CFG["reorder"].get(order[unit])
+                if eng is None or unit in reordered:
+                    continue
+                t, half = place(unit)
+                dst = re_pool.tile([LANES, 512], F32, name="re", tag="re", align_bytes=64)
+                reordered[unit] = dst
+                op = nc.scalar.copy if eng == "S" else nc.vector.tensor_copy
+                op(
+                    out=dst[:].rearrange("p (a v r) -> p a v r", a=2, v=2),
+                    in_=t[:].bitcast(F32)[:, 512 * half : 512 * half + 512].rearrange("p (a r v) -> p a v r", a=2, v=2),
+                )
 
         def transpose_units(count):
+            reorder(count)
             taken = units[:count]
             for unit in taken:
                 units.remove(unit)
-                job, half = unit
-                if half == 0:
-                    groups[job] = grp_pool.tile([LANES, 2048], BF16, name="grp", tag="grp", align_bytes=64)
+                t, half = place(unit)
+                words = t[:].bitcast(F32)[:, 512 * half : 512 * half + 512]
                 tp = psum.tile([LANES, 512], F32, name="tp", tag="tp")
-                blocks = job_blocks(job)[2 * half : 2 * half + 2]
-                for a, (t, base) in enumerate(blocks):
-                    words = t[:].bitcast(F32)
+                for a in range(2):
                     for v in range(2):
-                        nc.tensor.transpose(
-                            tp[:, 256 * a + 128 * v : 256 * a + 128 * v + 128],
-                            words[:, base + v : base + 256 : 2],
-                            ident[:],
-                        )
-                gw = groups[job][:].bitcast(F32)[:, 512 * half : 512 * half + 512]
+                        if unit in reordered:
+                            src = reordered[unit][:, 256 * a + 128 * v : 256 * a + 128 * v + 128]
+                        else:
+                            src = words[:, 256 * a + v : 256 * a + 256 : 2]
+                        nc.tensor.transpose(tp[:, 256 * a + 128 * v : 256 * a + 128 * v + 128], src, ident[:])
                 nc.scalar.copy(
-                    out=gw.rearrange("p (a r v) -> p a r v", a=2, v=2),
+                    out=words.rearrange("p (a r v) -> p a r v", a=2, v=2),
                     in_=tp[:].rearrange("p (a v r) -> p a r v", a=2, v=2),
                 )
-                if half == 1:
-                    ready.append(job)
+                to_quant.append(unit)
+            reorder(CFG["re_ahead"])
 
-        def quantize_ready():
-            for job in list(ready):
-                ready.remove(job)
-                codes, scales = job_target(job)
-                quantize(codes, scales, groups[job][:])
-
-        def interleave(eng_copy, grouped, raw, lo, hi):
-            eng_copy(
-                out=grouped[:].rearrange("p (d j) -> p d j", j=4)[:, lo:hi, :],
-                in_=raw[:].rearrange("p (j d) -> p d j", j=4)[:, lo:hi, :],
-            )
-
-        def grp_tile():
-            return grp_pool.tile([LANES, 2048], BF16, name="grp", tag="wgrp", bufs=2, align_bytes=64)
+        def quantize_units(count):
+            for unit in to_quant[:count]:
+                to_quant.remove(unit)
+                codes, scales = target(unit)
+                t, half = place(unit)
+                quantize(codes, scales, t[:, 1024 * half : 1024 * half + 1024])
 
         R_RE, R_IM, R_NEG = 0, 1, 2
 
-        def r_cols(which, lo=0, width=512):
+        def r_cols(which, lo, width):
             return slice(512 * which + lo, 512 * which + lo + width)
 
-        transpose_units(2)
-        g_rr = grp_tile()
-        interleave(nc.vector.tensor_copy, g_rr, raws[("r", "re")], 0, 512)
-        quantize_ready()
-        quantize(r_codes[:, r_cols(R_RE)], r_scales[:, r_cols(R_RE)], g_rr[:])
-        transpose_units(2)
-        g_ri = grp_tile()
-        interleave(nc.vector.tensor_copy, g_ri, raws[("r", "im")], 0, 352)
-        interleave(nc.scalar.copy, g_ri, raws[("r", "im")], 352, 512)
-        quantize_ready()
-        quantize(r_codes[:, r_cols(R_IM)], r_scales[:, r_cols(R_IM)], g_ri[:])
-        g_rn = grp_tile()
-        nc.vector.tensor_scalar(out=g_rn[:], in0=g_ri[:], scalar1=-1.0, scalar2=None, op0=ALU.mult)
-        transpose_units(4)
-        quantize(r_codes[:, r_cols(R_NEG)], r_scales[:, r_cols(R_NEG)], g_rn[:])
+        def mix_interleave(name, half):
+            t = raws[("r", name)][:, 1024 * half : 1024 * half + 1024].rearrange("p (j d) -> p d j", j=4)
+            grouped = wgrp_pool.tile([LANES, 1024], BF16, name="r_grp", tag="r_grp", align_bytes=64)
+            gview = grouped[:].rearrange("p (d j) -> p d j", j=4)
+            split = CFG["ri_split"] if name == "im" and half == 0 else 256
+            if half == 1 and CFG["r1_" + name] == "S":
+                nc.scalar.copy(out=gview, in_=t)
+                return grouped
+            nc.vector.tensor_copy(out=gview[:, 0:split, :], in_=t[:, 0:split, :])
+            if split < 256:
+                nc.scalar.copy(out=gview[:, split:256, :], in_=t[:, split:256, :])
+            return grouped
 
-        bias_ps = psum.tile([LANES, 512], F32, name="bias_ps", tag="acc")
-        nc.tensor.matmul(bias_ps[:], lhsT=ones[:], rhs=bias_row[:], start=True, stop=True)
-        nc.scalar.copy(out=bias_sb[:], in_=bias_ps[:])
+        def mix_quantize(which, half, grouped):
+            cols = r_cols(which, 256 * half, 256)
+            quantize(r_codes[:, cols], r_scales[:, cols], grouped[:])
+
+        def negate(grouped, half):
+            neg = wgrp_pool.tile([LANES, 1024], BF16, name="n_grp", tag="n_grp", bufs=2, align_bytes=64)
+            if CFG["neg_eng"][half] == "S":
+                nc.scalar.activation(out=neg[:], in_=grouped[:], func=ACT.Copy, scale=-1.0)
+            else:
+                nc.vector.tensor_scalar(out=neg[:], in0=grouped[:], scalar1=-1.0, scalar2=None, op0=ALU.mult)
+            return neg
 
         xq = (x_codes, x_scales)
         rq = (r_codes, r_scales)
@@ -240,15 +278,21 @@ def tile_fourier_operator_mix_f4_kernel(
         pending_add = []
         z_ready = []
 
-        def emit_adds():
-            for g, dq, prods in list(pending_add):
-                pending_add.remove((g, dq, prods))
-                a, b, c, e = prods
+        def emit_adds(engine_name):
+            for entry in list(pending_add):
+                i, prods = entry
+                g, dq = i // 4, i % 4
                 cols = slice(512 * dq, 512 * dq + 512)
-                nc.gpsimd.tensor_tensor(out=z_groups[("re", g)][:, cols], in0=a[:], in1=b[:], op=ALU.subtract)
-                nc.gpsimd.tensor_tensor(out=z_groups[("im", g)][:, cols], in0=c[:], in1=e[:], op=ALU.subtract)
-                if dq == 3:
-                    z_ready.append(g)
+                for name, flags, first, second in (("re", "g_re", prods[0], prods[1]), ("im", "g_im", prods[2], prods[3])):
+                    on_g = CFG[flags][i]
+                    if (engine_name == "G") != bool(on_g):
+                        continue
+                    eng = nc.gpsimd if on_g else nc.vector
+                    eng.tensor_tensor(out=z_groups[(name, g)][:, cols], in0=first[:], in1=second[:], op=ALU.subtract)
+                if engine_name == "V":
+                    pending_add.remove(entry)
+                    if dq == 3:
+                        z_ready.append(g)
 
         def quantize_z():
             for g in list(z_ready):
@@ -257,7 +301,8 @@ def tile_fourier_operator_mix_f4_kernel(
                     cols = slice(512 * (2 * s + g), 512 * (2 * s + g) + 512)
                     quantize(z_codes[:, cols], z_scales[:, cols], z_groups[(name, g)][:])
 
-        def stage1(g, dq):
+        def stage1(i):
+            g, dq = i // 4, i % 4
             if dq == 0:
                 for name in ("re", "im"):
                     z_groups[(name, g)] = zgrp_pool.tile([LANES, 2048], BF16, name="z_" + name, tag="z_" + name, align_bytes=64)
@@ -283,28 +328,54 @@ def tile_fourier_operator_mix_f4_kernel(
             gr = raws[("g", "re", g)][:].rearrange("p (t d) -> p d t", t=4)[:, 128 * dq : 128 * dq + 128, :]
             gi = raws[("g", "im", g)][:].rearrange("p (t d) -> p d t", t=4)[:, 128 * dq : 128 * dq + 128, :]
             nc.vector.scalar_tensor_tensor(out=spread(c), in0=yiv, scalar=-1.0, in1=gr, op0=ALU.mult, op1=ALU.mult)
-            nc.vector.tensor_tensor(out=spread(b), in0=yiv, in1=gi, op=ALU.mult)
             nc.vector.tensor_tensor(out=spread(a), in0=yrv, in1=gr, op=ALU.mult)
+            nc.vector.tensor_tensor(out=spread(b), in0=yiv, in1=gi, op=ALU.mult)
             nc.vector.tensor_tensor(out=spread(e), in0=yrv, in1=gi, op=ALU.mult)
-            pending_add.append((g, dq, (a, b, c, e)))
+            pending_add.append((i, (a, b, c, e)))
 
-        for i in range(8):
-            stage1(i // 4, i % 4)
-            transpose_units(3)
-            emit_adds()
-            quantize_ready()
+        transpose_units(2)
+        g_rr = mix_interleave("re", 0)
+        quantize_units(2)
+        mix_quantize(R_RE, 0, g_rr)
+        transpose_units(2)
+        g_ri = mix_interleave("im", 0)
+        quantize_units(2)
+        mix_quantize(R_IM, 0, g_ri)
+        g_rn = negate(g_ri, 0)
+        mix_quantize(R_NEG, 0, g_rn)
+        stage1(0)
+        g_rr = mix_interleave("re", 1)
+        g_ri = mix_interleave("im", 1)
+        mix_quantize(R_RE, 1, g_rr)
+        mix_quantize(R_IM, 1, g_ri)
+        g_rn = negate(g_ri, 1)
+        emit_adds("G")
+        emit_adds("V")
+        mix_quantize(R_NEG, 1, g_rn)
+        transpose_units(CFG["head_t"])
+        bias_ps = psum.tile([LANES, 512], F32, name="bias_ps", tag="acc")
+        nc.tensor.matmul(bias_ps[:], lhsT=ones[:], rhs=bias_row[:], start=True, stop=True)
+        nc.scalar.copy(out=bias_sb[:], in_=bias_ps[:])
+
+        for i in range(1, 8):
+            stage1(i)
+            emit_adds("G")
+            if i == 3 or i == 7:
+                pass
+            transpose_units(CFG["t_run"][i])
             quantize_z()
-            if i == 0:
-                load(4)
-            elif i == 3:
-                load(4)
-            elif i == 4:
-                load(4)
-            if i == 5:
-                g_w = grp_tile()
-                interleave(nc.scalar.copy, g_w, raws[("w",)], 0, 512)
-            if i == 6:
+            quantize_units(CFG["q_run"][i])
+            emit_adds("V")
+            if i == CFG["w_step"]:
+                g_w = wgrp_pool.tile([LANES, 2048], BF16, name="w_grp", tag="w_grp", bufs=1, align_bytes=64)
+                wop = nc.scalar.copy if CFG["w_eng"] == "S" else nc.vector.tensor_copy
+                wop(out=g_w[:].rearrange("p (d j) -> p d j", j=4), in_=raws[("w",)][:].rearrange("p (j d) -> p d j", j=4))
+            if i == CFG["w_step"] + 1:
                 quantize(w_codes[:], w_scales[:], g_w[:])
+            if i == 1:
+                load(40)
+        quantize_units(CFG["q_first"])
+        quantize_z()
 
         pending_gelu = []
 
@@ -316,10 +387,23 @@ def tile_fourier_operator_mix_f4_kernel(
                     q, j = n // 4, n % 4
                     nc.sync.dma_start(out=ov[q][:, j - 1 : j + 1, :], in_=o[:].rearrange("p (a d) -> p a d", a=2))
 
+        def ready_for(n):
+            need = [("cos", n), ("sin", n), ("u", n // 4, (n % 4) // 2)]
+            return not any(unit in to_quant for unit in need)
+
+        def transposed(n):
+            need = [("cos", n), ("sin", n), ("u", n // 4, (n % 4) // 2)]
+            return not any(unit in units for unit in need)
+
         for k in range(8):
-            transpose_units(4)
+            transpose_units(CFG["t_pair"][k])
             accs = []
+            o = out_pool.tile([LANES, 1024], F32, name="o", tag="o", bufs=3)
             for n in (2 * k, 2 * k + 1):
+                while not transposed(n):
+                    transpose_units(1)
+                while not ready_for(n):
+                    quantize_units(1)
                 acc = psum.tile([LANES, 512], F32, name="acc", tag="acc")
                 bq = basis_codes[n]
                 mx(acc[:], uq, slice(128 * n, 128 * n + 128), wq, slice(0, 512), True, False)
@@ -327,11 +411,18 @@ def tile_fourier_operator_mix_f4_kernel(
                     for g in range(2):
                         mx(acc[:], bq, slice(256 * s + 128 * g, 256 * s + 128 * g + 128), zq, slice(1024 * s + 512 * g, 1024 * s + 512 * g + 512), False, s == 1 and g == 1)
                 accs.append((n, acc))
-            quantize_ready()
             emit_gelu()
-            o = out_pool.tile([LANES, 1024], F32, name="o", tag="o")
             for n, acc in accs:
+                ahead = n + 2
+                if ahead < 16:
+                    while len(to_quant) and not ready_for(ahead):
+                        quantize_units(1)
                 v = out_pool.tile([LANES, 512], F32, name="v", tag="v")
-                nc.vector.tensor_tensor(out=v[:], in0=acc[:], in1=bias_sb[:], op=ALU.add)
+                if CFG["bias_g"][n]:
+                    raw_v = out_pool.tile([LANES, 512], F32, name="rv", tag="rv", bufs=2)
+                    nc.scalar.copy(out=raw_v[:], in_=acc[:])
+                    nc.gpsimd.tensor_tensor(out=v[:], in0=raw_v[:], in1=bias_sb[:], op=ALU.add)
+                else:
+                    nc.vector.tensor_tensor(out=v[:], in0=acc[:], in1=bias_sb[:], op=ALU.add)
                 pending_gelu.append((n, v, o))
         emit_gelu()

@@ -19,19 +19,25 @@ LANES = 128
 CFG = {
     "raw_bufs": 24,
     "b_bufs": 8,
-    "t_run": [5,5,5,5,5,5,5,5],
-    "t_pair": [2,2,2,2,2,2,2,2],
-    "q_run": [4,4,1,1,1,1,1,1],
+    "t_run": [0,5,4,4,4,4,4,7],
+    "t_pair": [4,4,4,4,4,4,4,4],
+    "q_run": [0,0,4,1,1,1,1,1],
     "q_first": 1,
+    "q_pos": [0,0,0,0,0,0,0,0],
+    "zq_pos": 0,
     "g_re": [0,0,0,0,0,0,0,0],
-    "g_im": [0,0,0,0,0,0,0,0],
-    "reorder": {},
-    "re_ahead": 3,
-    "head_t": 4,
-    "w_step": 4,
+    "g_im": [1,1,1,1,1,1,1,0],
+    "reorder": {10: "S", 13: "S", 16: "S", 19: "S", 22: "S", 25: "S", 28: "S", 31: "S", 33: "V", 35: "V", 37: "V", 39: "V", 41: "V", 43: "V", 45: "V", 47: "V"},
+    "re_ahead": 5,
+    "re_pos": 0,
+    "re_bufs": 4,
+    "head_t": 3,
+    "w_step": 5,
     "w_eng": "S",
     "ri_split": 256,
-    "bias_g": [0,0,0,0,0,0,0,0,0,0,0,0,0,0,0,0],
+    "warm": 0,
+    "warm2": 3,
+    "bias_g": [0,0,1,0,0,0,1,0,0,0,1,0,0,0,1,0],
     "r1_re": "S",
     "r1_im": "S",
     "neg_eng": ["V","V"],
@@ -51,7 +57,7 @@ def tile_fourier_operator_mix_f4_kernel(
         basis_pool = ctx.enter_context(tc.tile_pool(name="basis", bufs=CFG["b_bufs"]))
         prod_pool = ctx.enter_context(tc.tile_pool(name="prod", bufs=2))
         out_pool = ctx.enter_context(tc.tile_pool(name="outs", bufs=2))
-        re_pool = ctx.enter_context(tc.tile_pool(name="reord", bufs=5))
+        re_pool = ctx.enter_context(tc.tile_pool(name="reord", bufs=CFG["re_bufs"]))
         psum = ctx.enter_context(tc.psum_pool(name="psum", bufs=4))
 
         xv = {
@@ -73,7 +79,7 @@ def tile_fourier_operator_mix_f4_kernel(
 
         sources = [
             ("x", "re", 0, 0), ("x", "re", 0, 1), ("r", "re", 0), ("x", "im", 0, 0), ("x", "im", 0, 1), ("r", "im", 0),
-            ("g", "re", 0), ("g", "im", 0), ("r", "re", 1), ("r", "im", 1),
+            ("r", "re", 1), ("r", "im", 1), ("g", "re", 0), ("g", "im", 0),
             ("x", "re", 1, 0), ("x", "re", 1, 1), ("x", "im", 1, 0), ("x", "im", 1, 1),
             ("cos", 0, 0), ("sin", 0, 0), ("u", 0), ("cos", 0, 1), ("sin", 0, 1),
             ("g", "re", 1), ("g", "im", 1), ("w",),
@@ -121,6 +127,8 @@ def tile_fourier_operator_mix_f4_kernel(
         nc.scalar.activation(out=warm[:], in_=dummy[:], func=ACT.Gelu_apprx_tanh)
         ones = keep.tile([LANES, LANES], BF16, name="ones")
         nc.vector.memset(ones[:], 1.0)
+        zeros = keep.tile([LANES, D], BF16, name="zeros")
+        nc.vector.memset(zeros[:], 0.0)
         bias_row = keep.tile([LANES, D], BF16, name="bias_row")
         nc.vector.memset(bias_row[:], 0.0)
         nc.scalar.dma_start(out=bias_row[0:1, :], in_=bias.unsqueeze(0))
@@ -209,7 +217,7 @@ def tile_fourier_operator_mix_f4_kernel(
                     in_=t[:].bitcast(F32)[:, 512 * half : 512 * half + 512].rearrange("p (a r v) -> p a v r", a=2, v=2),
                 )
 
-        def transpose_units(count):
+        def transpose_units(count, follow=True):
             reorder(count)
             taken = units[:count]
             for unit in taken:
@@ -229,7 +237,8 @@ def tile_fourier_operator_mix_f4_kernel(
                     in_=tp[:].rearrange("p (a v r) -> p a r v", a=2, v=2),
                 )
                 to_quant.append(unit)
-            reorder(CFG["re_ahead"])
+            if follow:
+                reorder(CFG["re_ahead"])
 
         def quantize_units(count):
             for unit in to_quant[:count]:
@@ -333,29 +342,33 @@ def tile_fourier_operator_mix_f4_kernel(
             nc.vector.tensor_tensor(out=spread(e), in0=yrv, in1=gi, op=ALU.mult)
             pending_add.append((i, (a, b, c, e)))
 
+        def keep_warm(count):
+            if count:
+                idle_ps = psum.tile([LANES, 512], F32, name="idle_ps", tag="tp")
+            for step in range(count):
+                nc.tensor.matmul(idle_ps[:], lhsT=ones[:], rhs=zeros[:], start=True, stop=True)
+
+        keep_warm(CFG["warm"])
         transpose_units(2)
         g_rr = mix_interleave("re", 0)
-        quantize_units(2)
+        quantize_units(1)
         mix_quantize(R_RE, 0, g_rr)
+        quantize_units(1)
         transpose_units(2)
+        keep_warm(CFG["warm2"])
         g_ri = mix_interleave("im", 0)
-        quantize_units(2)
-        mix_quantize(R_IM, 0, g_ri)
+        quantize_units(1)
         g_rn = negate(g_ri, 0)
+        quantize_units(1)
+        mix_quantize(R_IM, 0, g_ri)
         mix_quantize(R_NEG, 0, g_rn)
-        stage1(0)
         g_rr = mix_interleave("re", 1)
         g_ri = mix_interleave("im", 1)
+        stage1(0)
         mix_quantize(R_RE, 1, g_rr)
-        mix_quantize(R_IM, 1, g_ri)
         g_rn = negate(g_ri, 1)
-        emit_adds("G")
-        emit_adds("V")
+        mix_quantize(R_IM, 1, g_ri)
         mix_quantize(R_NEG, 1, g_rn)
-        transpose_units(CFG["head_t"])
-        bias_ps = psum.tile([LANES, 512], F32, name="bias_ps", tag="acc")
-        nc.tensor.matmul(bias_ps[:], lhsT=ones[:], rhs=bias_row[:], start=True, stop=True)
-        nc.scalar.copy(out=bias_sb[:], in_=bias_ps[:])
 
         for i in range(1, 8):
             stage1(i)
@@ -374,29 +387,37 @@ def tile_fourier_operator_mix_f4_kernel(
                 quantize(w_codes[:], w_scales[:], g_w[:])
             if i == 1:
                 load(40)
+            if i == 2:
+                bias_ps = psum.tile([LANES, 512], F32, name="bias_ps", tag="tp")
+                nc.tensor.matmul(bias_ps[:], lhsT=ones[:], rhs=bias_row[:], start=True, stop=True)
+                nc.scalar.copy(out=bias_sb[:], in_=bias_ps[:])
         quantize_units(CFG["q_first"])
         quantize_z()
 
         pending_gelu = []
 
         def emit_gelu():
-            for n, v, o in list(pending_gelu):
-                pending_gelu.remove((n, v, o))
-                nc.scalar.activation(out=o[:, 512 * (n % 2) : 512 * (n % 2) + 512], in_=v[:], func=ACT.Gelu_apprx_tanh)
-                if n % 2 == 1:
-                    q, j = n // 4, n % 4
+            for n, lo, hi, v, o in list(pending_gelu):
+                pending_gelu.remove((n, lo, hi, v, o))
+                q, j = n // 4, n % 4
+                base = 512 * (n % 2)
+                nc.scalar.activation(out=o[:, base + lo : base + hi], in_=v[:, lo:hi], func=ACT.Gelu_apprx_tanh)
+                if n >= 14:
+                    nc.sync.dma_start(out=ov[q][:, j, lo:hi], in_=o[:, base + lo : base + hi])
+                elif n % 2 == 1:
                     nc.sync.dma_start(out=ov[q][:, j - 1 : j + 1, :], in_=o[:].rearrange("p (a d) -> p a d", a=2))
 
+        def unit_needs(n):
+            return [("cos", n), ("sin", n), ("u", n // 4, (n % 4) // 2)]
+
         def ready_for(n):
-            need = [("cos", n), ("sin", n), ("u", n // 4, (n % 4) // 2)]
-            return not any(unit in to_quant for unit in need)
+            return not any(unit in to_quant for unit in unit_needs(n))
 
         def transposed(n):
-            need = [("cos", n), ("sin", n), ("u", n // 4, (n % 4) // 2)]
-            return not any(unit in units for unit in need)
+            return not any(unit in units for unit in unit_needs(n))
 
         for k in range(8):
-            transpose_units(CFG["t_pair"][k])
+            transpose_units(CFG["t_pair"][k], False)
             accs = []
             o = out_pool.tile([LANES, 1024], F32, name="o", tag="o", bufs=3)
             for n in (2 * k, 2 * k + 1):
@@ -404,25 +425,23 @@ def tile_fourier_operator_mix_f4_kernel(
                     transpose_units(1)
                 while not ready_for(n):
                     quantize_units(1)
-                acc = psum.tile([LANES, 512], F32, name="acc", tag="acc")
                 bq = basis_codes[n]
-                mx(acc[:], uq, slice(128 * n, 128 * n + 128), wq, slice(0, 512), True, False)
-                for s in range(2):
-                    for g in range(2):
-                        mx(acc[:], bq, slice(256 * s + 128 * g, 256 * s + 128 * g + 128), zq, slice(1024 * s + 512 * g, 1024 * s + 512 * g + 512), False, s == 1 and g == 1)
-                accs.append((n, acc))
+                for lo, hi in ((0, 256), (256, 512)) if n == 15 else ((0, 512),):
+                    acc = psum.tile([LANES, 512], F32, name="acc", tag="acc")
+                    mx(acc[:, 0 : hi - lo], uq, slice(128 * n, 128 * n + 128), wq, slice(lo, hi), True, False)
+                    for s in range(2):
+                        for g in range(2):
+                            mx(acc[:, 0 : hi - lo], bq, slice(256 * s + 128 * g, 256 * s + 128 * g + 128), zq, slice(1024 * s + 512 * g + lo, 1024 * s + 512 * g + hi), False, s == 1 and g == 1)
+                    accs.append((n, lo, hi, acc))
             emit_gelu()
-            for n, acc in accs:
+            reorder(CFG["re_ahead"])
+            for n, lo, hi, acc in accs:
                 ahead = n + 2
-                if ahead < 16:
+                if ahead < 16 and lo == 0:
                     while len(to_quant) and not ready_for(ahead):
                         quantize_units(1)
-                v = out_pool.tile([LANES, 512], F32, name="v", tag="v")
-                if CFG["bias_g"][n]:
-                    raw_v = out_pool.tile([LANES, 512], F32, name="rv", tag="rv", bufs=2)
-                    nc.scalar.copy(out=raw_v[:], in_=acc[:])
-                    nc.gpsimd.tensor_tensor(out=v[:], in0=raw_v[:], in1=bias_sb[:], op=ALU.add)
-                else:
-                    nc.vector.tensor_tensor(out=v[:], in0=acc[:], in1=bias_sb[:], op=ALU.add)
-                pending_gelu.append((n, v, o))
+                if lo == 0:
+                    v = out_pool.tile([LANES, 512], F32, name="v", tag="v", bufs=3)
+                nc.vector.tensor_tensor(out=v[:, lo:hi], in0=acc[:, 0 : hi - lo], in1=bias_sb[:, lo:hi], op=ALU.add)
+                pending_gelu.append((n, lo, hi, v, o))
         emit_gelu()

@@ -19,28 +19,33 @@ LANES = 128
 CFG = {
     "raw_bufs": 24,
     "b_bufs": 8,
-    "t_run": [0,5,4,4,4,4,4,7],
-    "t_pair": [4,4,4,4,4,4,4,4],
-    "q_run": [0,0,4,1,1,1,1,1],
-    "q_first": 1,
+    "t_run": [0,5,4,4,4,4,4,4],
+    "t_pair": [8,8,8,8,8,8,8,8],
+    "q_run": [0,2,0,0,0,0,0,0],
+    "q_first": 4,
     "q_pos": [0,0,0,0,0,0,0,0],
     "zq_pos": 0,
-    "g_re": [0,0,0,0,0,0,0,0],
+    "g_re": [1,1,1,1,1,1,1,0],
     "g_im": [1,1,1,1,1,1,1,0],
-    "reorder": {10: "S", 13: "S", 16: "S", 19: "S", 22: "S", 25: "S", 28: "S", 31: "S", 33: "V", 35: "V", 37: "V", 39: "V", 41: "V", 43: "V", 45: "V", 47: "V"},
-    "re_ahead": 5,
+    "reorder": {37: "S", 39: "S", 41: "S", 43: "S", 45: "S", 47: "S"},
+    "re_ahead": 4,
     "re_pos": 0,
     "re_bufs": 4,
     "head_t": 3,
-    "w_step": 5,
+    "w_step": 3,
     "w_eng": "S",
-    "ri_split": 256,
+    "ri_split": 192,
     "warm": 0,
-    "warm2": 3,
-    "bias_g": [0,0,1,0,0,0,1,0,0,0,1,0,0,0,1,0],
+    "warm2": 5,
+    "yi_first": 1,
+    "w_early": 0,
+    "m2_group": 2,
+    "v_bufs": 3,
+    "split": [0,2,2,2,2,2,2,2],
+    "bias_g": [0,0,0,0,0,0,0,0,0,0,0,0,0,0,0,0],
     "r1_re": "S",
     "r1_im": "S",
-    "neg_eng": ["V","V"],
+    "neg_eng": ["S","S"],
 }
 
 
@@ -84,6 +89,9 @@ def tile_fourier_operator_mix_f4_kernel(
             ("cos", 0, 0), ("sin", 0, 0), ("u", 0), ("cos", 0, 1), ("sin", 0, 1),
             ("g", "re", 1), ("g", "im", 1), ("w",),
         ]
+        if CFG["w_early"]:
+            sources.remove(("w",))
+            sources.insert(14, ("w",))
         for q in range(1, 4):
             sources += [("cos", q, 0), ("sin", q, 0), ("u", q), ("cos", q, 1), ("sin", q, 1)]
         raws = {}
@@ -166,13 +174,10 @@ def tile_fourier_operator_mix_f4_kernel(
         for part in range(2):
             units.append(("x", "im", 0, part))
         units += [("x", name, 1, part) for name in ("re", "im") for part in range(2)]
-        units += [("cos", 0), ("sin", 0), ("cos", 1), ("sin", 1)]
-        units += [("u", 0, 0), ("u", 0, 1), ("cos", 2), ("sin", 2), ("cos", 3), ("sin", 3)]
-        for q in range(1, 4):
-            for j in range(4):
-                if j == 2:
-                    units += [("u", q, 0), ("u", q, 1)]
-                units += [("cos", 4 * q + j), ("sin", 4 * q + j)]
+        for q in range(4):
+            units += [("cos", 4 * q), ("cos", 4 * q + 1), ("sin", 4 * q), ("sin", 4 * q + 1)]
+            units += [("u", q, 0), ("u", q, 1)]
+            units += [("cos", 4 * q + 2), ("cos", 4 * q + 3), ("sin", 4 * q + 2), ("sin", 4 * q + 3)]
         order = {unit: i for i, unit in enumerate(units)}
         to_quant = []
         reordered = {}
@@ -189,19 +194,15 @@ def tile_fourier_operator_mix_f4_kernel(
         def target(unit):
             kind = unit[0]
             if kind == "x":
-                c = 1024 * (unit[1] == "im") + 512 * unit[2] + 256 * unit[3]
-                return x_codes[:, c : c + 256], x_scales[:, c : c + 256]
+                c = 1024 * (unit[1] == "im") + 512 * unit[2]
+                return x_codes[:, c : c + 512], x_scales[:, c : c + 512]
             if kind == "u":
-                c = 512 * unit[1] + 256 * unit[2]
-                return u_codes[:, c : c + 256], u_scales[:, c : c + 256]
-            n = unit[1]
-            if n not in basis_codes:
-                codes = basis_pool.tile([LANES, 512], U32, name="b_codes", tag="b_codes", align_bytes=64)
-                scales = basis_pool.tile([LANES, 512], U8, name="b_scales", tag="b_scales", align_bytes=64)
-                basis_codes[n] = (codes, scales)
-            codes, scales = basis_codes[n]
-            c = 256 * (kind == "sin")
-            return codes[:, c : c + 256], scales[:, c : c + 256]
+                c = 512 * unit[1]
+                return u_codes[:, c : c + 512], u_scales[:, c : c + 512]
+            codes = basis_pool.tile([LANES, 512], U32, name="b_codes", tag="b_codes", align_bytes=64)
+            scales = basis_pool.tile([LANES, 512], U8, name="b_scales", tag="b_scales", align_bytes=64)
+            basis_codes[(kind, unit[1] // 2)] = (codes, scales)
+            return codes[:], scales[:]
 
         def reorder(count):
             for unit in units[:count]:
@@ -211,6 +212,16 @@ def tile_fourier_operator_mix_f4_kernel(
                 t, half = place(unit)
                 dst = re_pool.tile([LANES, 512], F32, name="re", tag="re", align_bytes=64)
                 reordered[unit] = dst
+                if eng == "G":
+                    nc.gpsimd.tensor_scalar(
+                        out=dst[:].bitcast(BF16).rearrange("p (a v r e) -> p a v r e", a=2, v=2, e=2),
+                        in0=t[:, 1024 * half : 1024 * half + 1024].rearrange("p (a r v e) -> p a v r e", a=2, v=2, e=2),
+                        scalar1=1.0,
+                        scalar2=0.0,
+                        op0=ALU.mult,
+                        op1=ALU.add,
+                    )
+                    continue
                 op = nc.scalar.copy if eng == "S" else nc.vector.tensor_copy
                 op(
                     out=dst[:].rearrange("p (a v r) -> p a v r", a=2, v=2),
@@ -236,7 +247,8 @@ def tile_fourier_operator_mix_f4_kernel(
                     out=words.rearrange("p (a r v) -> p a r v", a=2, v=2),
                     in_=tp[:].rearrange("p (a v r) -> p a r v", a=2, v=2),
                 )
-                to_quant.append(unit)
+                if half == 1:
+                    to_quant.append(unit)
             if follow:
                 reorder(CFG["re_ahead"])
 
@@ -245,7 +257,7 @@ def tile_fourier_operator_mix_f4_kernel(
                 to_quant.remove(unit)
                 codes, scales = target(unit)
                 t, half = place(unit)
-                quantize(codes, scales, t[:, 1024 * half : 1024 * half + 1024])
+                quantize(codes, scales, t[:])
 
         R_RE, R_IM, R_NEG = 0, 1, 2
 
@@ -297,7 +309,12 @@ def tile_fourier_operator_mix_f4_kernel(
                     if (engine_name == "G") != bool(on_g):
                         continue
                     eng = nc.gpsimd if on_g else nc.vector
-                    eng.tensor_tensor(out=z_groups[(name, g)][:, cols], in0=first[:], in1=second[:], op=ALU.subtract)
+                    eng.tensor_tensor(
+                        out=z_groups[(name, g)][:, cols].rearrange("p (n t) -> p n t", t=4),
+                        in0=first[:].rearrange("p (t n) -> p n t", t=4),
+                        in1=second[:].rearrange("p (t n) -> p n t", t=4),
+                        op=ALU.subtract,
+                    )
                 if engine_name == "V":
                     pending_add.remove(entry)
                     if dq == 3:
@@ -310,7 +327,7 @@ def tile_fourier_operator_mix_f4_kernel(
                     cols = slice(512 * (2 * s + g), 512 * (2 * s + g) + 512)
                     quantize(z_codes[:, cols], z_scales[:, cols], z_groups[(name, g)][:])
 
-        def stage1(i):
+        def stage1(i, between=0):
             g, dq = i // 4, i % 4
             if dq == 0:
                 for name in ("re", "im"):
@@ -324,22 +341,26 @@ def tile_fourier_operator_mix_f4_kernel(
                     im_cols = slice(1024 + 512 * g + 128 * t, 1024 + 512 * g + 128 * t + 128)
                     mx(o, xq, re_cols, rq, r_cols(first, 128 * dq, 128), True, False)
                     mx(o, xq, im_cols, rq, r_cols(second, 128 * dq, 128), False, True)
+                if acc is yi:
+                    transpose_units(between)
             a = prod_pool.tile([LANES, 512], F32, name="pa", tag="pa")
             b = prod_pool.tile([LANES, 512], F32, name="pb", tag="pb")
             c = prod_pool.tile([LANES, 512], F32, name="pc", tag="pc")
             e = prod_pool.tile([LANES, 512], F32, name="pe", tag="pe")
 
-            def spread(t):
-                return t[:].rearrange("p (n t) -> p n t", t=4)
+            def by_slot(t):
+                return t[:].rearrange("p (t n) -> p t n", t=4)
 
-            yiv = yi[:].rearrange("p (t n) -> p n t", t=4)
-            yrv = yr[:].rearrange("p (t n) -> p n t", t=4)
-            gr = raws[("g", "re", g)][:].rearrange("p (t d) -> p d t", t=4)[:, 128 * dq : 128 * dq + 128, :]
-            gi = raws[("g", "im", g)][:].rearrange("p (t d) -> p d t", t=4)[:, 128 * dq : 128 * dq + 128, :]
-            nc.vector.scalar_tensor_tensor(out=spread(c), in0=yiv, scalar=-1.0, in1=gr, op0=ALU.mult, op1=ALU.mult)
-            nc.vector.tensor_tensor(out=spread(a), in0=yrv, in1=gr, op=ALU.mult)
-            nc.vector.tensor_tensor(out=spread(b), in0=yiv, in1=gi, op=ALU.mult)
-            nc.vector.tensor_tensor(out=spread(e), in0=yrv, in1=gi, op=ALU.mult)
+            cols = slice(128 * dq, 128 * dq + 128)
+            gr = raws[("g", "re", g)][:].rearrange("p (t d) -> p t d", t=4)[:, :, cols]
+            gi = raws[("g", "im", g)][:].rearrange("p (t d) -> p t d", t=4)[:, :, cols]
+            nc.vector.scalar_tensor_tensor(out=by_slot(c), in0=by_slot(yi), scalar=-1.0, in1=gr, op0=ALU.mult, op1=ALU.mult)
+            for step in range(2):
+                if (step == 0) == bool(CFG["yi_first"]):
+                    nc.vector.tensor_tensor(out=by_slot(b), in0=by_slot(yi), in1=gi, op=ALU.mult)
+                else:
+                    nc.vector.tensor_tensor(out=by_slot(a), in0=by_slot(yr), in1=gr, op=ALU.mult)
+            nc.vector.tensor_tensor(out=by_slot(e), in0=by_slot(yr), in1=gi, op=ALU.mult)
             pending_add.append((i, (a, b, c, e)))
 
         def keep_warm(count):
@@ -353,13 +374,11 @@ def tile_fourier_operator_mix_f4_kernel(
         g_rr = mix_interleave("re", 0)
         quantize_units(1)
         mix_quantize(R_RE, 0, g_rr)
-        quantize_units(1)
         transpose_units(2)
         keep_warm(CFG["warm2"])
         g_ri = mix_interleave("im", 0)
         quantize_units(1)
         g_rn = negate(g_ri, 0)
-        quantize_units(1)
         mix_quantize(R_IM, 0, g_ri)
         mix_quantize(R_NEG, 0, g_rn)
         g_rr = mix_interleave("re", 1)
@@ -371,18 +390,25 @@ def tile_fourier_operator_mix_f4_kernel(
         mix_quantize(R_NEG, 1, g_rn)
 
         for i in range(1, 8):
-            stage1(i)
+            split = CFG["split"][i]
+            stage1(i, split)
             emit_adds("G")
             if i == 3 or i == 7:
                 pass
-            transpose_units(CFG["t_run"][i])
+            transpose_units(CFG["t_run"][i] - split)
             quantize_z()
             quantize_units(CFG["q_run"][i])
             emit_adds("V")
             if i == CFG["w_step"]:
                 g_w = wgrp_pool.tile([LANES, 2048], BF16, name="w_grp", tag="w_grp", bufs=1, align_bytes=64)
-                wop = nc.scalar.copy if CFG["w_eng"] == "S" else nc.vector.tensor_copy
-                wop(out=g_w[:].rearrange("p (d j) -> p d j", j=4), in_=raws[("w",)][:].rearrange("p (j d) -> p d j", j=4))
+                w_out = g_w[:].rearrange("p (d j) -> p d j", j=4)
+                w_in = raws[("w",)][:].rearrange("p (j d) -> p d j", j=4)
+                if CFG["w_eng"] == "G":
+                    nc.gpsimd.tensor_scalar(out=w_out, in0=w_in, scalar1=1.0, scalar2=0.0, op0=ALU.mult, op1=ALU.add)
+                elif CFG["w_eng"] == "S":
+                    nc.scalar.copy(out=w_out, in_=w_in)
+                else:
+                    nc.vector.tensor_copy(out=w_out, in_=w_in)
             if i == CFG["w_step"] + 1:
                 quantize(w_codes[:], w_scales[:], g_w[:])
             if i == 1:
@@ -408,7 +434,8 @@ def tile_fourier_operator_mix_f4_kernel(
                     nc.sync.dma_start(out=ov[q][:, j - 1 : j + 1, :], in_=o[:].rearrange("p (a d) -> p a d", a=2))
 
         def unit_needs(n):
-            return [("cos", n), ("sin", n), ("u", n // 4, (n % 4) // 2)]
+            odd = n + 1 - n % 2
+            return [("cos", odd), ("sin", odd), ("u", n // 4, 1)]
 
         def ready_for(n):
             return not any(unit in to_quant for unit in unit_needs(n))
@@ -416,32 +443,40 @@ def tile_fourier_operator_mix_f4_kernel(
         def transposed(n):
             return not any(unit in units for unit in unit_needs(n))
 
-        for k in range(8):
+        group = CFG["m2_group"]
+        for k in range(8 // group):
             transpose_units(CFG["t_pair"][k], False)
             accs = []
-            o = out_pool.tile([LANES, 1024], F32, name="o", tag="o", bufs=3)
-            for n in (2 * k, 2 * k + 1):
+            for n in range(2 * group * k, 2 * group * (k + 1)):
                 while not transposed(n):
                     transpose_units(1)
                 while not ready_for(n):
                     quantize_units(1)
-                bq = basis_codes[n]
                 for lo, hi in ((0, 256), (256, 512)) if n == 15 else ((0, 512),):
                     acc = psum.tile([LANES, 512], F32, name="acc", tag="acc")
                     mx(acc[:, 0 : hi - lo], uq, slice(128 * n, 128 * n + 128), wq, slice(lo, hi), True, False)
                     for s in range(2):
                         for g in range(2):
-                            mx(acc[:, 0 : hi - lo], bq, slice(256 * s + 128 * g, 256 * s + 128 * g + 128), zq, slice(1024 * s + 512 * g + lo, 1024 * s + 512 * g + hi), False, s == 1 and g == 1)
+                            bq = basis_codes[(("cos", "sin")[s], n // 2)]
+                            bc = 256 * (n % 2) + 128 * g
+                            mx(acc[:, 0 : hi - lo], bq, slice(bc, bc + 128), zq, slice(1024 * s + 512 * g + lo, 1024 * s + 512 * g + hi), False, s == 1 and g == 1)
                     accs.append((n, lo, hi, acc))
             emit_gelu()
             reorder(CFG["re_ahead"])
             for n, lo, hi, acc in accs:
-                ahead = n + 2
+                ahead = 2 * group * (k + 1) + (n % (2 * group)) // 2 * 2
                 if ahead < 16 and lo == 0:
                     while len(to_quant) and not ready_for(ahead):
                         quantize_units(1)
                 if lo == 0:
-                    v = out_pool.tile([LANES, 512], F32, name="v", tag="v", bufs=3)
-                nc.vector.tensor_tensor(out=v[:, lo:hi], in0=acc[:, 0 : hi - lo], in1=bias_sb[:, lo:hi], op=ALU.add)
+                    v = out_pool.tile([LANES, 512], F32, name="v", tag="v", bufs=CFG["v_bufs"])
+                    if n % 2 == 0:
+                        o = out_pool.tile([LANES, 1024], F32, name="o", tag="o", bufs=3)
+                if CFG["bias_g"][n]:
+                    raw_v = out_pool.tile([LANES, 512], F32, name="rv", tag="rv", bufs=2)
+                    nc.scalar.copy(out=raw_v[:], in_=acc[:])
+                    nc.gpsimd.tensor_tensor(out=v[:], in0=raw_v[:], in1=bias_sb[:], op=ALU.add)
+                else:
+                    nc.vector.tensor_tensor(out=v[:, lo:hi], in0=acc[:, 0 : hi - lo], in1=bias_sb[:, lo:hi], op=ALU.add)
                 pending_gelu.append((n, lo, hi, v, o))
         emit_gelu()

@@ -16,37 +16,24 @@ ALU = mybir.AluOpType
 ACT = mybir.ActivationFunctionType
 
 LANES = 128
-CFG = {
-    "raw_bufs": 24,
-    "b_bufs": 8,
-    "t_run": [0,5,4,4,4,4,4,4],
-    "t_pair": [8,8,8,8,8,8,8,8],
-    "q_run": [0,2,0,0,0,0,0,0],
-    "q_first": 4,
-    "q_pos": [0,0,0,0,0,0,0,0],
-    "zq_pos": 0,
-    "g_re": [1,1,1,1,1,1,1,0],
-    "g_im": [1,1,1,1,1,1,1,0],
-    "reorder": {37: "S", 39: "S", 41: "S", 43: "S", 45: "S", 47: "S"},
-    "re_ahead": 4,
-    "re_pos": 0,
-    "re_bufs": 4,
-    "head_t": 3,
-    "w_step": 3,
-    "w_eng": "S",
-    "ri_split": 192,
-    "warm": 0,
-    "warm2": 5,
-    "yi_first": 1,
-    "w_early": 0,
-    "m2_group": 2,
-    "v_bufs": 3,
-    "split": [0,2,2,2,2,2,2,2],
-    "bias_g": [0,0,0,0,0,0,0,0,0,0,0,0,0,0,0,0],
-    "r1_re": "S",
-    "r1_im": "S",
-    "neg_eng": ["S","S"],
-}
+PACK = 4
+RAW = 2048
+HALF = RAW // 2
+WORDS = 512
+UNITS = 8
+QUARTER = D // 4
+
+RAW_BUFS = 24
+FIRST_LOADS = 30
+
+TURN_BETWEEN = 2
+TURN_AFTER = (0, 2, 2, 2, 2, 2, 2, 4)
+TURN_STAGE_2 = 5
+SORT_FROM = 36
+SORT_AHEAD = 5
+
+R_IM_SPLIT = 208
+IDLE_MATMULS = 4
 
 
 def tile_fourier_operator_mix_f4_kernel(
@@ -55,77 +42,54 @@ def tile_fourier_operator_mix_f4_kernel(
     nc = tc.nc
     with ExitStack() as ctx:
         ctx.enter_context(tc.manual_schedule())
-        raw_pool = ctx.enter_context(tc.tile_pool(name="raw", bufs=CFG["raw_bufs"]))
+        raw_pool = ctx.enter_context(tc.tile_pool(name="raw", bufs=RAW_BUFS))
         keep = ctx.enter_context(tc.tile_pool(name="keep", bufs=1))
-        wgrp_pool = ctx.enter_context(tc.tile_pool(name="wgrp", bufs=3))
-        zgrp_pool = ctx.enter_context(tc.tile_pool(name="zgrp", bufs=1))
-        basis_pool = ctx.enter_context(tc.tile_pool(name="basis", bufs=CFG["b_bufs"]))
-        prod_pool = ctx.enter_context(tc.tile_pool(name="prod", bufs=2))
-        out_pool = ctx.enter_context(tc.tile_pool(name="outs", bufs=2))
-        re_pool = ctx.enter_context(tc.tile_pool(name="reord", bufs=CFG["re_bufs"]))
+        mix_pool = ctx.enter_context(tc.tile_pool(name="mix", bufs=3))
+        z_pool = ctx.enter_context(tc.tile_pool(name="z", bufs=1))
+        basis_pool = ctx.enter_context(tc.tile_pool(name="basis", bufs=6))
+        product_pool = ctx.enter_context(tc.tile_pool(name="product", bufs=2))
+        out_pool = ctx.enter_context(tc.tile_pool(name="result", bufs=3))
+        sort_pool = ctx.enter_context(tc.tile_pool(name="sort", bufs=6))
         psum = ctx.enter_context(tc.psum_pool(name="psum", bufs=4))
 
-        xv = {
-            "re": x_re.rearrange("(g m t) k -> g m t k", g=2, t=4),
-            "im": x_im.rearrange("(g m t) k -> g m t k", g=2, t=4),
+        views = {
+            "x_re": [x_re.rearrange("(g m t) k -> g m t k", g=2, t=4)[g] for g in range(2)],
+            "x_im": [x_im.rearrange("(g m t) k -> g m t k", g=2, t=4)[g] for g in range(2)],
+            "g_re": [g_re.rearrange("(g m t) d -> g m t d", g=2, t=4)[g] for g in range(2)],
+            "g_im": [g_im.rearrange("(g m t) d -> g m t d", g=2, t=4)[g] for g in range(2)],
+            "r_re": [r_re.rearrange("(p j) d -> p j d", j=PACK)],
+            "r_im": [r_im.rearrange("(p j) d -> p j d", j=PACK)],
+            "w": [w.rearrange("(p j) d -> p j d", j=PACK)],
+            "u": [u.rearrange("(q p j) k -> q p j k", q=4, j=4)[q] for q in range(4)],
+            "cos": [basis_cos.rearrange("(q p j) k -> q p j k", q=4, j=4)[m // 2][:, 2 * (m % 2) : 2 * (m % 2) + 2, :] for m in range(8)],
+            "sin": [basis_sin.rearrange("(q p j) k -> q p j k", q=4, j=4)[m // 2][:, 2 * (m % 2) : 2 * (m % 2) + 2, :] for m in range(8)],
         }
-        gv = {
-            "re": g_re.rearrange("(g m t) d -> g m t d", g=2, t=4),
-            "im": g_im.rearrange("(g m t) d -> g m t d", g=2, t=4),
-        }
-        bv = {
-            "cos": basis_cos.rearrange("(q p j) k -> q p j k", q=4, j=4),
-            "sin": basis_sin.rearrange("(q p j) k -> q p j k", q=4, j=4),
-        }
-        uv = u.rearrange("(q p j) k -> q p j k", q=4, j=4)
-        ov = out.rearrange("(q p j) d -> q p j d", q=4, j=4)
-        rv = {"re": r_re.rearrange("(p j) d -> p j d", j=4), "im": r_im.rearrange("(p j) d -> p j d", j=4)}
-        wv = w.rearrange("(p j) d -> p j d", j=4)
+        out_view = out.rearrange("(q p j) d -> q p j d", q=4, j=4)
 
-        sources = [
-            ("x", "re", 0, 0), ("x", "re", 0, 1), ("r", "re", 0), ("x", "im", 0, 0), ("x", "im", 0, 1), ("r", "im", 0),
-            ("r", "re", 1), ("r", "im", 1), ("g", "re", 0), ("g", "im", 0),
-            ("x", "re", 1, 0), ("x", "re", 1, 1), ("x", "im", 1, 0), ("x", "im", 1, 1),
-            ("cos", 0, 0), ("sin", 0, 0), ("u", 0), ("cos", 0, 1), ("sin", 0, 1),
-            ("g", "re", 1), ("g", "im", 1), ("w",),
-        ]
-        if CFG["w_early"]:
-            sources.remove(("w",))
-            sources.insert(14, ("w",))
-        for q in range(1, 4):
-            sources += [("cos", q, 0), ("sin", q, 0), ("u", q), ("cos", q, 1), ("sin", q, 1)]
-        raws = {}
+        loads = [("x_re", 0, 0), ("x_re", 0, 1), ("r_re", 0, 0), ("x_im", 0, 0), ("x_im", 0, 1), ("r_im", 0, 0)]
+        loads += [("r_re", 0, 1), ("r_im", 0, 1), ("g_re", 0, None), ("g_im", 0, None)]
+        loads += [("x_re", 1, 0), ("x_re", 1, 1), ("x_im", 1, 0), ("x_im", 1, 1), ("g_re", 1, None), ("g_im", 1, None)]
+        for q in range(4):
+            loads += [("cos", 2 * q, None), ("sin", 2 * q, None), ("u", q, None), ("cos", 2 * q + 1, None), ("sin", 2 * q + 1, None)]
+            if q == 0:
+                loads += [("w", 0, None)]
+        raw = {}
 
-        def load(count):
-            for step in range(count):
-                if not sources:
-                    return
-                key = sources[0]
-                sources.remove(key)
-                kind = key[0]
-                part = None
-                base = key
-                if kind == "x":
-                    base, part = key[:3], key[3]
-                    src = xv[key[1]][key[2]][:, 2 * part : 2 * part + 2, :]
-                elif kind == "g":
-                    src = gv[key[1]][key[2]]
-                elif kind == "r":
-                    base, part = key[:2], key[2]
-                    src = rv[key[1]][:, :, 256 * part : 256 * part + 256]
-                elif kind == "w":
-                    src = wv
-                elif kind == "u":
-                    src = uv[key[1]]
-                else:
-                    src = bv[kind][key[1]][:, 2 * key[2] : 2 * key[2] + 2, :]
-                if base not in raws:
-                    raws[base] = raw_pool.tile([LANES, 2048], BF16, name="raw", tag="raw", align_bytes=64)
-                t = raws[base]
-                dst = t[:] if part is None else t[:, 1024 * part : 1024 * part + 1024]
+        def load(entries):
+            for name, index, part in entries:
+                src = views[name][index]
+                if (name, index) not in raw:
+                    raw[(name, index)] = raw_pool.tile([LANES, RAW], BF16, name="raw", align_bytes=64)
+                dst = raw[(name, index)][:]
+                if part is not None:
+                    dst = dst[:, HALF * part : HALF * part + HALF]
+                    if name in ("x_re", "x_im"):
+                        src = src[:, 2 * part : 2 * part + 2, :]
+                    else:
+                        src = src[:, :, 256 * part : 256 * part + 256]
                 nc.sync.dma_start(out=dst.rearrange("p (a b) -> p a b", a=src.shape[1]), in_=src)
 
-        load(22 + CFG["raw_bufs"] - 16)
+        load(loads[:FIRST_LOADS])
 
         ident = keep.tile([LANES, LANES], F32, name="ident")
         make_identity(nc, ident[:])
@@ -140,343 +104,271 @@ def tile_fourier_operator_mix_f4_kernel(
         bias_row = keep.tile([LANES, D], BF16, name="bias_row")
         nc.vector.memset(bias_row[:], 0.0)
         nc.scalar.dma_start(out=bias_row[0:1, :], in_=bias.unsqueeze(0))
-        bias_sb = keep.tile([LANES, D], F32, name="bias_sb")
+        bias_all = keep.tile([LANES, D], F32, name="bias_all")
 
-        x_codes = keep.tile([LANES, 4 * 512], U32, name="x_codes", align_bytes=64)
-        x_scales = keep.tile([LANES, 4 * 512], U8, name="x_scales", align_bytes=64)
-        r_codes = keep.tile([LANES, 3 * 512], U32, name="r_codes", align_bytes=64)
-        r_scales = keep.tile([LANES, 3 * 512], U8, name="r_scales", align_bytes=64)
-        w_codes = keep.tile([LANES, 512], U32, name="w_codes", align_bytes=64)
-        w_scales = keep.tile([LANES, 512], U8, name="w_scales", align_bytes=64)
-        z_codes = keep.tile([LANES, 4 * 512], U32, name="z_codes", align_bytes=64)
-        z_scales = keep.tile([LANES, 4 * 512], U8, name="z_scales", align_bytes=64)
-        u_codes = keep.tile([LANES, 4 * 512], U32, name="u_codes", align_bytes=64)
-        u_scales = keep.tile([LANES, 4 * 512], U8, name="u_scales", align_bytes=64)
-        basis_codes = {}
+        def quantised(columns, name):
+            codes = keep.tile([LANES, columns], U32, name=name + "_codes", align_bytes=64)
+            scales = keep.tile([LANES, columns], U8, name=name + "_scales", align_bytes=64)
+            return codes, scales
 
-        def quantize(codes, scales, grouped):
-            nc.vector.quantize_mx(out=codes.bitcast(FP8X4), scales=scales, in_=grouped)
+        x_q = quantised(4 * 512, "x")
+        r_q = quantised(3 * 512, "r")
+        w_q = quantised(512, "w")
+        z_q = quantised(4 * 512, "z")
+        u_q = quantised(4 * 512, "u")
+        basis_q = {}
+        R_RE, R_IM, R_NEG = 0, 512, 1024
 
-        def mx(acc, lhs, lhs_cols, rhs, rhs_cols, start, stop):
+        def quantize(operand, first, columns, grouped):
+            codes, scales = operand
+            nc.vector.quantize_mx(
+                out=codes[:, first : first + columns].bitcast(FP8X4),
+                scales=scales[:, first : first + columns],
+                in_=grouped,
+            )
+
+        def mx(acc, stationary, s_first, moving, m_first, columns, start, stop):
             nc.tensor.matmul_mx(
                 out=acc,
-                lhsT=lhs[0][:, lhs_cols].bitcast(FP8X4),
-                lhsT_scale=lhs[1][:, lhs_cols],
-                rhs=rhs[0][:, rhs_cols].bitcast(FP8X4),
-                rhs_scale=rhs[1][:, rhs_cols],
+                lhsT=stationary[0][:, s_first : s_first + LANES].bitcast(FP8X4),
+                lhsT_scale=stationary[1][:, s_first : s_first + LANES],
+                rhs=moving[0][:, m_first : m_first + columns].bitcast(FP8X4),
+                rhs_scale=moving[1][:, m_first : m_first + columns],
                 start=start,
                 stop=stop,
             )
 
-        units = []
-        for part in range(2):
-            units.append(("x", "re", 0, part))
-        for part in range(2):
-            units.append(("x", "im", 0, part))
-        units += [("x", name, 1, part) for name in ("re", "im") for part in range(2)]
+        to_turn = [(name, g, half) for g in range(2) for name in ("x_re", "x_im") for half in range(2)]
         for q in range(4):
-            units += [("cos", 4 * q), ("cos", 4 * q + 1), ("sin", 4 * q), ("sin", 4 * q + 1)]
-            units += [("u", q, 0), ("u", q, 1)]
-            units += [("cos", 4 * q + 2), ("cos", 4 * q + 3), ("sin", 4 * q + 2), ("sin", 4 * q + 3)]
-        order = {unit: i for i, unit in enumerate(units)}
-        to_quant = []
-        reordered = {}
+            for name, index in (("cos", 2 * q), ("sin", 2 * q), ("u", q), ("cos", 2 * q + 1), ("sin", 2 * q + 1)):
+                to_turn += [(name, index, half) for half in range(2)]
+        to_sort = [unit for i, unit in enumerate(to_turn) if i >= SORT_FROM and i % 3 != 0]
+        sorted_words = {}
+        to_quantize = []
 
-        def place(unit):
-            kind = unit[0]
-            if kind == "x":
-                return raws[unit[:3]], unit[3]
-            if kind == "u":
-                return raws[unit[:2]], unit[2]
-            n = unit[1]
-            return raws[(kind, n // 4, (n % 4) // 2)], n % 2
+        def raw_words(name, index, half):
+            return raw[(name, index)][:].bitcast(F32)[:, WORDS * half : WORDS * half + WORDS]
 
-        def target(unit):
-            kind = unit[0]
-            if kind == "x":
-                c = 1024 * (unit[1] == "im") + 512 * unit[2]
-                return x_codes[:, c : c + 512], x_scales[:, c : c + 512]
-            if kind == "u":
-                c = 512 * unit[1]
-                return u_codes[:, c : c + 512], u_scales[:, c : c + 512]
-            codes = basis_pool.tile([LANES, 512], U32, name="b_codes", tag="b_codes", align_bytes=64)
-            scales = basis_pool.tile([LANES, 512], U8, name="b_scales", tag="b_scales", align_bytes=64)
-            basis_codes[(kind, unit[1] // 2)] = (codes, scales)
-            return codes[:], scales[:]
-
-        def reorder(count):
-            for unit in units[:count]:
-                eng = CFG["reorder"].get(order[unit])
-                if eng is None or unit in reordered:
-                    continue
-                t, half = place(unit)
-                dst = re_pool.tile([LANES, 512], F32, name="re", tag="re", align_bytes=64)
-                reordered[unit] = dst
-                if eng == "G":
-                    nc.gpsimd.tensor_scalar(
-                        out=dst[:].bitcast(BF16).rearrange("p (a v r e) -> p a v r e", a=2, v=2, e=2),
-                        in0=t[:, 1024 * half : 1024 * half + 1024].rearrange("p (a r v e) -> p a v r e", a=2, v=2, e=2),
-                        scalar1=1.0,
-                        scalar2=0.0,
-                        op0=ALU.mult,
-                        op1=ALU.add,
+        def sort_ahead():
+            for unit in to_turn[:SORT_AHEAD]:
+                if unit in to_sort:
+                    to_sort.remove(unit)
+                    dst = sort_pool.tile([LANES, WORDS], F32, name="sorted", align_bytes=64)
+                    nc.scalar.copy(
+                        out=dst[:].rearrange("p (a e r) -> p a e r", a=2, e=2),
+                        in_=raw_words(*unit).rearrange("p (a r e) -> p a e r", a=2, e=2),
                     )
-                    continue
-                op = nc.scalar.copy if eng == "S" else nc.vector.tensor_copy
-                op(
-                    out=dst[:].rearrange("p (a v r) -> p a v r", a=2, v=2),
-                    in_=t[:].bitcast(F32)[:, 512 * half : 512 * half + 512].rearrange("p (a r v) -> p a v r", a=2, v=2),
-                )
+                    sorted_words[unit] = dst
 
-        def transpose_units(count, follow=True):
-            reorder(count)
-            taken = units[:count]
-            for unit in taken:
-                units.remove(unit)
-                t, half = place(unit)
-                words = t[:].bitcast(F32)[:, 512 * half : 512 * half + 512]
-                tp = psum.tile([LANES, 512], F32, name="tp", tag="tp")
+        def turn(count):
+            for unit in to_turn[:count]:
+                to_turn.remove(unit)
+                words = raw_words(*unit)
+                bank = psum.tile([LANES, WORDS], F32, name="turned")
                 for a in range(2):
-                    for v in range(2):
-                        if unit in reordered:
-                            src = reordered[unit][:, 256 * a + 128 * v : 256 * a + 128 * v + 128]
+                    for e in range(2):
+                        first = 256 * a + 128 * e
+                        if unit in sorted_words:
+                            src = sorted_words[unit][:, first : first + 128]
                         else:
-                            src = words[:, 256 * a + v : 256 * a + 256 : 2]
-                        nc.tensor.transpose(tp[:, 256 * a + 128 * v : 256 * a + 128 * v + 128], src, ident[:])
+                            src = words[:, 256 * a + e : 256 * a + 256 : 2]
+                        nc.tensor.transpose(bank[:, first : first + 128], src, ident[:])
                 nc.scalar.copy(
-                    out=words.rearrange("p (a r v) -> p a r v", a=2, v=2),
-                    in_=tp[:].rearrange("p (a v r) -> p a r v", a=2, v=2),
+                    out=words.rearrange("p (a r e) -> p a r e", a=2, e=2),
+                    in_=bank[:].rearrange("p (a e r) -> p a r e", a=2, e=2),
                 )
+                name, index, half = unit
                 if half == 1:
-                    to_quant.append(unit)
-            if follow:
-                reorder(CFG["re_ahead"])
+                    to_quantize.append((name, index))
 
-        def quantize_units(count):
-            for unit in to_quant[:count]:
-                to_quant.remove(unit)
-                codes, scales = target(unit)
-                t, half = place(unit)
-                quantize(codes, scales, t[:])
+        def quantize_turned(count):
+            for name, index in to_quantize[:count]:
+                to_quantize.remove((name, index))
+                if name in ("x_re", "x_im"):
+                    operand, first = x_q, 1024 * (name == "x_im") + 512 * index
+                elif name == "u":
+                    operand, first = u_q, 512 * index
+                else:
+                    codes = basis_pool.tile([LANES, 512], U32, name="basis_codes", align_bytes=64)
+                    scales = basis_pool.tile([LANES, 512], U8, name="basis_scales", align_bytes=64)
+                    basis_q[(name, index)] = (codes, scales)
+                    operand, first = basis_q[(name, index)], 0
+                quantize(operand, first, 512, raw[(name, index)][:])
 
-        R_RE, R_IM, R_NEG = 0, 1, 2
-
-        def r_cols(which, lo, width):
-            return slice(512 * which + lo, 512 * which + lo + width)
-
-        def mix_interleave(name, half):
-            t = raws[("r", name)][:, 1024 * half : 1024 * half + 1024].rearrange("p (j d) -> p d j", j=4)
-            grouped = wgrp_pool.tile([LANES, 1024], BF16, name="r_grp", tag="r_grp", align_bytes=64)
-            gview = grouped[:].rearrange("p (d j) -> p d j", j=4)
-            split = CFG["ri_split"] if name == "im" and half == 0 else 256
-            if half == 1 and CFG["r1_" + name] == "S":
-                nc.scalar.copy(out=gview, in_=t)
-                return grouped
-            nc.vector.tensor_copy(out=gview[:, 0:split, :], in_=t[:, 0:split, :])
-            if split < 256:
-                nc.scalar.copy(out=gview[:, split:256, :], in_=t[:, split:256, :])
+        def interleave_r(name, half):
+            src = raw[(name, 0)][:, HALF * half : HALF * half + HALF].rearrange("p (j d) -> p d j", j=PACK)
+            grouped = mix_pool.tile([LANES, HALF], BF16, name="r_grouped", align_bytes=64)
+            dst = grouped[:].rearrange("p (d j) -> p d j", j=PACK)
+            on_vector = (256 if name == "r_re" else R_IM_SPLIT) if half == 0 else 0
+            if on_vector > 0:
+                nc.vector.tensor_copy(out=dst[:, :on_vector, :], in_=src[:, :on_vector, :])
+            if on_vector < 256:
+                nc.scalar.copy(out=dst[:, on_vector:, :], in_=src[:, on_vector:, :])
             return grouped
 
-        def mix_quantize(which, half, grouped):
-            cols = r_cols(which, 256 * half, 256)
-            quantize(r_codes[:, cols], r_scales[:, cols], grouped[:])
+        def negate(grouped):
+            negative = mix_pool.tile([LANES, HALF], BF16, name="r_negative", bufs=2, align_bytes=64)
+            nc.scalar.activation(out=negative[:], in_=grouped[:], func=ACT.Copy, scale=-1.0)
+            return negative
 
-        def negate(grouped, half):
-            neg = wgrp_pool.tile([LANES, 1024], BF16, name="n_grp", tag="n_grp", bufs=2, align_bytes=64)
-            if CFG["neg_eng"][half] == "S":
-                nc.scalar.activation(out=neg[:], in_=grouped[:], func=ACT.Copy, scale=-1.0)
+        def quantize_r(part, half, grouped):
+            quantize(r_q, part + 256 * half, 256, grouped[:])
+
+        packed_gain = {name: keep.tile([LANES, RAW], BF16, name="packed_" + name, align_bytes=64) for name in ("g_re", "g_im")}
+        w_grouped = keep.tile([LANES, RAW], BF16, name="w_grouped", align_bytes=64)
+        pieces = [(packed_gain[name], (name, 1), i) for i in range(4) for name in ("g_re", "g_im")]
+        pieces += [(w_grouped, ("w", 0), i) for i in range(4)]
+
+        def by_column(tile):
+            return tile[:].rearrange("p (t n) -> p n t", t=4)
+
+        def interleaved(tile):
+            return tile[:].rearrange("p (n t) -> p n t", t=4)
+
+        def copy_piece():
+            for dst, key, i in pieces[:1]:
+                pieces.remove((dst, key, i))
+                columns = slice(QUARTER * i, QUARTER * i + QUARTER)
+                nc.scalar.copy(out=interleaved(dst)[:, columns, :], in_=by_column(raw[key])[:, columns, :])
+
+        z_rounded = {}
+        products = {}
+
+        def mix(i, name):
+            g, columns = i // 4, QUARTER * (i % 4)
+            first, second = (R_IM, R_RE) if name == "y_im" else (R_RE, R_NEG)
+            acc = psum.tile([LANES, WORDS], F32, name=name, tag="acc")
+            for t in range(4):
+                slot = acc[:, 128 * t : 128 * t + 128]
+                mx(slot, x_q, 512 * g + 128 * t, r_q, first + columns, QUARTER, True, False)
+                mx(slot, x_q, 1024 + 512 * g + 128 * t, r_q, second + columns, QUARTER, False, True)
+            return acc
+
+        def multiply_gains(i, y_im, y_re):
+            g = i // 4
+            columns = slice(QUARTER * (i % 4), QUARTER * (i % 4) + QUARTER)
+            if g == 0:
+                gain_re, gain_im = by_column(raw[("g_re", 0)])[:, columns, :], by_column(raw[("g_im", 0)])[:, columns, :]
             else:
-                nc.vector.tensor_scalar(out=neg[:], in0=grouped[:], scalar1=-1.0, scalar2=None, op0=ALU.mult)
-            return neg
+                gain_re, gain_im = interleaved(packed_gain["g_re"])[:, columns, :], interleaved(packed_gain["g_im"])[:, columns, :]
+            re_re = product_pool.tile([LANES, WORDS], F32, name="re_re")
+            im_im = product_pool.tile([LANES, WORDS], F32, name="im_im")
+            minus_re_im = product_pool.tile([LANES, WORDS], F32, name="minus_re_im")
+            im_re = product_pool.tile([LANES, WORDS], F32, name="im_re")
+            nc.vector.scalar_tensor_tensor(
+                out=interleaved(minus_re_im), in0=by_column(y_im), scalar=-1.0, in1=gain_re, op0=ALU.mult, op1=ALU.mult
+            )
+            nc.vector.tensor_tensor(out=interleaved(im_im), in0=by_column(y_im), in1=gain_im, op=ALU.mult)
+            nc.vector.tensor_tensor(out=interleaved(re_re), in0=by_column(y_re), in1=gain_re, op=ALU.mult)
+            nc.vector.tensor_tensor(out=interleaved(im_re), in0=by_column(y_re), in1=gain_im, op=ALU.mult)
+            products[i] = {"z_re": (re_re, im_im), "minus_z_im": (minus_re_im, im_re)}
 
-        xq = (x_codes, x_scales)
-        rq = (r_codes, r_scales)
-        wq = (w_codes, w_scales)
-        zq = (z_codes, z_scales)
-        uq = (u_codes, u_scales)
+        def subtract(i, engine):
+            g, first = i // 4, WORDS * (i % 4)
+            for name, (left, right) in products[i].items():
+                if (name, g) not in z_rounded:
+                    z_rounded[(name, g)] = z_pool.tile([LANES, RAW], BF16, name=name, align_bytes=64)
+                engine.tensor_tensor(
+                    out=z_rounded[(name, g)][:, first : first + WORDS], in0=left[:], in1=right[:], op=ALU.subtract
+                )
 
-        z_groups = {}
-        pending_add = []
-        z_ready = []
+        def quantize_z(g):
+            quantize(z_q, 512 * g, 512, z_rounded[("z_re", g)][:])
+            quantize(z_q, 1024 + 512 * g, 512, z_rounded[("minus_z_im", g)][:])
 
-        def emit_adds(engine_name):
-            for entry in list(pending_add):
-                i, prods = entry
-                g, dq = i // 4, i % 4
-                cols = slice(512 * dq, 512 * dq + 512)
-                for name, flags, first, second in (("re", "g_re", prods[0], prods[1]), ("im", "g_im", prods[2], prods[3])):
-                    on_g = CFG[flags][i]
-                    if (engine_name == "G") != bool(on_g):
-                        continue
-                    eng = nc.gpsimd if on_g else nc.vector
-                    eng.tensor_tensor(
-                        out=z_groups[(name, g)][:, cols].rearrange("p (n t) -> p n t", t=4),
-                        in0=first[:].rearrange("p (t n) -> p n t", t=4),
-                        in1=second[:].rearrange("p (t n) -> p n t", t=4),
-                        op=ALU.subtract,
-                    )
-                if engine_name == "V":
-                    pending_add.remove(entry)
-                    if dq == 3:
-                        z_ready.append(g)
+        turn(2)
+        r_re_grouped = interleave_r("r_re", 0)
+        quantize_turned(1)
+        quantize_r(R_RE, 0, r_re_grouped)
+        turn(2)
+        idle = psum.tile([LANES, WORDS], F32, name="idle", tag="turned")
+        for i in range(IDLE_MATMULS):
+            nc.tensor.matmul(idle[:], lhsT=ones[:], rhs=zeros[:], start=True, stop=True)
+        r_im_grouped = interleave_r("r_im", 0)
+        quantize_turned(1)
+        r_negative = negate(r_im_grouped)
+        quantize_r(R_IM, 0, r_im_grouped)
+        quantize_r(R_NEG, 0, r_negative)
+        r_re_grouped = interleave_r("r_re", 1)
+        r_im_grouped = interleave_r("r_im", 1)
+        y_im = mix(0, "y_im")
+        y_re = mix(0, "y_re")
+        multiply_gains(0, y_im, y_re)
+        quantize_r(R_RE, 1, r_re_grouped)
+        r_negative = negate(r_im_grouped)
+        quantize_r(R_IM, 1, r_im_grouped)
+        quantize_r(R_NEG, 1, r_negative)
 
-        def quantize_z():
-            for g in list(z_ready):
-                z_ready.remove(g)
-                for s, name in enumerate(("re", "im")):
-                    cols = slice(512 * (2 * s + g), 512 * (2 * s + g) + 512)
-                    quantize(z_codes[:, cols], z_scales[:, cols], z_groups[(name, g)][:])
-
-        def stage1(i, between=0):
-            g, dq = i // 4, i % 4
-            if dq == 0:
-                for name in ("re", "im"):
-                    z_groups[(name, g)] = zgrp_pool.tile([LANES, 2048], BF16, name="z_" + name, tag="z_" + name, align_bytes=64)
-            yi = psum.tile([LANES, 512], F32, name="yi", tag="acc")
-            yr = psum.tile([LANES, 512], F32, name="yr", tag="acc")
-            for acc, first, second in ((yi, R_IM, R_RE), (yr, R_RE, R_NEG)):
-                for t in range(4):
-                    o = acc[:, 128 * t : 128 * t + 128]
-                    re_cols = slice(512 * g + 128 * t, 512 * g + 128 * t + 128)
-                    im_cols = slice(1024 + 512 * g + 128 * t, 1024 + 512 * g + 128 * t + 128)
-                    mx(o, xq, re_cols, rq, r_cols(first, 128 * dq, 128), True, False)
-                    mx(o, xq, im_cols, rq, r_cols(second, 128 * dq, 128), False, True)
-                if acc is yi:
-                    transpose_units(between)
-            a = prod_pool.tile([LANES, 512], F32, name="pa", tag="pa")
-            b = prod_pool.tile([LANES, 512], F32, name="pb", tag="pb")
-            c = prod_pool.tile([LANES, 512], F32, name="pc", tag="pc")
-            e = prod_pool.tile([LANES, 512], F32, name="pe", tag="pe")
-
-            def by_slot(t):
-                return t[:].rearrange("p (t n) -> p t n", t=4)
-
-            cols = slice(128 * dq, 128 * dq + 128)
-            gr = raws[("g", "re", g)][:].rearrange("p (t d) -> p t d", t=4)[:, :, cols]
-            gi = raws[("g", "im", g)][:].rearrange("p (t d) -> p t d", t=4)[:, :, cols]
-            nc.vector.scalar_tensor_tensor(out=by_slot(c), in0=by_slot(yi), scalar=-1.0, in1=gr, op0=ALU.mult, op1=ALU.mult)
-            for step in range(2):
-                if (step == 0) == bool(CFG["yi_first"]):
-                    nc.vector.tensor_tensor(out=by_slot(b), in0=by_slot(yi), in1=gi, op=ALU.mult)
-                else:
-                    nc.vector.tensor_tensor(out=by_slot(a), in0=by_slot(yr), in1=gr, op=ALU.mult)
-            nc.vector.tensor_tensor(out=by_slot(e), in0=by_slot(yr), in1=gi, op=ALU.mult)
-            pending_add.append((i, (a, b, c, e)))
-
-        def keep_warm(count):
-            if count:
-                idle_ps = psum.tile([LANES, 512], F32, name="idle_ps", tag="tp")
-            for step in range(count):
-                nc.tensor.matmul(idle_ps[:], lhsT=ones[:], rhs=zeros[:], start=True, stop=True)
-
-        keep_warm(CFG["warm"])
-        transpose_units(2)
-        g_rr = mix_interleave("re", 0)
-        quantize_units(1)
-        mix_quantize(R_RE, 0, g_rr)
-        transpose_units(2)
-        keep_warm(CFG["warm2"])
-        g_ri = mix_interleave("im", 0)
-        quantize_units(1)
-        g_rn = negate(g_ri, 0)
-        mix_quantize(R_IM, 0, g_ri)
-        mix_quantize(R_NEG, 0, g_rn)
-        g_rr = mix_interleave("re", 1)
-        g_ri = mix_interleave("im", 1)
-        stage1(0)
-        mix_quantize(R_RE, 1, g_rr)
-        g_rn = negate(g_ri, 1)
-        mix_quantize(R_IM, 1, g_ri)
-        mix_quantize(R_NEG, 1, g_rn)
-
-        for i in range(1, 8):
-            split = CFG["split"][i]
-            stage1(i, split)
-            emit_adds("G")
-            if i == 3 or i == 7:
-                pass
-            transpose_units(CFG["t_run"][i] - split)
-            quantize_z()
-            quantize_units(CFG["q_run"][i])
-            emit_adds("V")
-            if i == CFG["w_step"]:
-                g_w = wgrp_pool.tile([LANES, 2048], BF16, name="w_grp", tag="w_grp", bufs=1, align_bytes=64)
-                w_out = g_w[:].rearrange("p (d j) -> p d j", j=4)
-                w_in = raws[("w",)][:].rearrange("p (j d) -> p d j", j=4)
-                if CFG["w_eng"] == "G":
-                    nc.gpsimd.tensor_scalar(out=w_out, in0=w_in, scalar1=1.0, scalar2=0.0, op0=ALU.mult, op1=ALU.add)
-                elif CFG["w_eng"] == "S":
-                    nc.scalar.copy(out=w_out, in_=w_in)
-                else:
-                    nc.vector.tensor_copy(out=w_out, in_=w_in)
-            if i == CFG["w_step"] + 1:
-                quantize(w_codes[:], w_scales[:], g_w[:])
+        for i in range(1, UNITS):
+            y_im = mix(i, "y_im")
+            turn(TURN_BETWEEN)
+            sort_ahead()
+            copy_piece()
+            y_re = mix(i, "y_re")
+            multiply_gains(i, y_im, y_re)
             if i == 1:
-                load(40)
+                subtract(0, nc.gpsimd)
+            if i < UNITS - 1:
+                subtract(i, nc.gpsimd)
+            turn(TURN_AFTER[i])
+            sort_ahead()
+            if i == 4:
+                quantize_z(0)
+            if i == 1:
+                quantize_turned(2)
+            if i == UNITS - 1:
+                subtract(i, nc.vector)
+            copy_piece()
+            if i == 1:
+                load(loads[FIRST_LOADS:])
             if i == 2:
-                bias_ps = psum.tile([LANES, 512], F32, name="bias_ps", tag="tp")
-                nc.tensor.matmul(bias_ps[:], lhsT=ones[:], rhs=bias_row[:], start=True, stop=True)
-                nc.scalar.copy(out=bias_sb[:], in_=bias_ps[:])
-        quantize_units(CFG["q_first"])
-        quantize_z()
+                bias_bank = psum.tile([LANES, WORDS], F32, name="bias_bank", tag="turned")
+                nc.tensor.matmul(bias_bank[:], lhsT=ones[:], rhs=bias_row[:], start=True, stop=True)
+                nc.scalar.copy(out=bias_all[:], in_=bias_bank[:])
+        quantize(w_q, 0, 512, w_grouped[:])
+        quantize_turned(3)
+        quantize_z(1)
 
-        pending_gelu = []
+        to_finish = []
 
-        def emit_gelu():
-            for n, lo, hi, v, o in list(pending_gelu):
-                pending_gelu.remove((n, lo, hi, v, o))
+        def finish():
+            for n, lo, hi, biased, result in list(to_finish):
+                to_finish.remove((n, lo, hi, biased, result))
+                base = D * (n % 2)
+                nc.scalar.activation(out=result[:, base + lo : base + hi], in_=biased[:, lo:hi], func=ACT.Gelu_apprx_tanh)
                 q, j = n // 4, n % 4
-                base = 512 * (n % 2)
-                nc.scalar.activation(out=o[:, base + lo : base + hi], in_=v[:, lo:hi], func=ACT.Gelu_apprx_tanh)
-                if n >= 14:
-                    nc.sync.dma_start(out=ov[q][:, j, lo:hi], in_=o[:, base + lo : base + hi])
+                if n >= N // LANES - 2:
+                    nc.sync.dma_start(out=out_view[q][:, j, lo:hi], in_=result[:, base + lo : base + hi])
                 elif n % 2 == 1:
-                    nc.sync.dma_start(out=ov[q][:, j - 1 : j + 1, :], in_=o[:].rearrange("p (a d) -> p a d", a=2))
+                    nc.sync.dma_start(out=out_view[q][:, j - 1 : j + 1, :], in_=result[:].rearrange("p (a d) -> p a d", a=2))
 
-        def unit_needs(n):
-            odd = n + 1 - n % 2
-            return [("cos", odd), ("sin", odd), ("u", n // 4, 1)]
+        def quantize_for(n):
+            needed = [("cos", n // 2), ("sin", n // 2), ("u", n // 4)]
+            while any(key in to_quantize for key in needed):
+                quantize_turned(1)
 
-        def ready_for(n):
-            return not any(unit in to_quant for unit in unit_needs(n))
-
-        def transposed(n):
-            return not any(unit in units for unit in unit_needs(n))
-
-        group = CFG["m2_group"]
-        for k in range(8 // group):
-            transpose_units(CFG["t_pair"][k], False)
-            accs = []
-            for n in range(2 * group * k, 2 * group * (k + 1)):
-                while not transposed(n):
-                    transpose_units(1)
-                while not ready_for(n):
-                    quantize_units(1)
-                for lo, hi in ((0, 256), (256, 512)) if n == 15 else ((0, 512),):
-                    acc = psum.tile([LANES, 512], F32, name="acc", tag="acc")
-                    mx(acc[:, 0 : hi - lo], uq, slice(128 * n, 128 * n + 128), wq, slice(lo, hi), True, False)
-                    for s in range(2):
+        for step in range(4):
+            turn(TURN_STAGE_2)
+            banks = []
+            for n in range(4 * step, 4 * step + 4):
+                quantize_for(n)
+                for lo, hi in ((0, 256), (256, 512)) if n == N // LANES - 1 else ((0, 512),):
+                    acc = psum.tile([LANES, WORDS], F32, name="field", tag="acc")
+                    sums = acc[:, 0 : hi - lo]
+                    mx(sums, u_q, LANES * n, w_q, lo, hi - lo, True, False)
+                    for s, name in enumerate(("cos", "sin")):
                         for g in range(2):
-                            bq = basis_codes[(("cos", "sin")[s], n // 2)]
-                            bc = 256 * (n % 2) + 128 * g
-                            mx(acc[:, 0 : hi - lo], bq, slice(bc, bc + 128), zq, slice(1024 * s + 512 * g + lo, 1024 * s + 512 * g + hi), False, s == 1 and g == 1)
-                    accs.append((n, lo, hi, acc))
-            emit_gelu()
-            reorder(CFG["re_ahead"])
-            for n, lo, hi, acc in accs:
-                ahead = 2 * group * (k + 1) + (n % (2 * group)) // 2 * 2
-                if ahead < 16 and lo == 0:
-                    while len(to_quant) and not ready_for(ahead):
-                        quantize_units(1)
+                            mx(sums, basis_q[(name, n // 2)], 256 * (n % 2) + 128 * g, z_q, 1024 * s + 512 * g + lo, hi - lo, False, s == 1 and g == 1)
+                    banks.append((n, lo, hi, sums))
+            finish()
+            sort_ahead()
+            for n, lo, hi, sums in banks:
+                if step < 3:
+                    quantize_for(n + 4)
                 if lo == 0:
-                    v = out_pool.tile([LANES, 512], F32, name="v", tag="v", bufs=CFG["v_bufs"])
+                    biased = out_pool.tile([LANES, D], F32, name="biased")
                     if n % 2 == 0:
-                        o = out_pool.tile([LANES, 1024], F32, name="o", tag="o", bufs=3)
-                if CFG["bias_g"][n]:
-                    raw_v = out_pool.tile([LANES, 512], F32, name="rv", tag="rv", bufs=2)
-                    nc.scalar.copy(out=raw_v[:], in_=acc[:])
-                    nc.gpsimd.tensor_tensor(out=v[:], in0=raw_v[:], in1=bias_sb[:], op=ALU.add)
-                else:
-                    nc.vector.tensor_tensor(out=v[:, lo:hi], in0=acc[:, 0 : hi - lo], in1=bias_sb[:, lo:hi], op=ALU.add)
-                pending_gelu.append((n, lo, hi, v, o))
-        emit_gelu()
+                        result = out_pool.tile([LANES, 2 * D], F32, name="result")
+                nc.vector.tensor_tensor(out=biased[:, lo:hi], in0=sums, in1=bias_all[:, lo:hi], op=ALU.add)
+                to_finish.append((n, lo, hi, biased, result))
+        finish()

from contextlib import ExitStack

import concourse.mybir as mybir
from concourse.masks import make_identity

N, P, C, D = 2048, 1024, 512, 512

FLOPS = 2 * (4 * P * C * D + 2 * N * P * D + N * C * D)

F32 = mybir.dt.float32
BF16 = mybir.dt.bfloat16
U32 = mybir.dt.uint32
U8 = mybir.dt.uint8
FP8X4 = mybir.dt.float8_e4m3fn_x4
ALU = mybir.AluOpType
ACT = mybir.ActivationFunctionType

LANES = 128
PACK = 4
RAW = 2048
HALF = RAW // 2
WORDS = 512
UNITS = 8
QUARTER = D // 4

RAW_BUFS = 24
FIRST_LOADS = 30

TURN_BETWEEN = 2
TURN_AFTER = (0, 2, 2, 2, 2, 2, 2, 4)
TURN_STAGE_2 = 5
SORT_FROM = 36
SORT_AHEAD = 5

R_IM_SPLIT = 208
IDLE_MATMULS = 4


def tile_fourier_operator_mix_f4_kernel(
    tc, x_re, x_im, r_re, r_im, g_re, g_im, basis_cos, basis_sin, u, w, bias, out
):
    nc = tc.nc
    with ExitStack() as ctx:
        ctx.enter_context(tc.manual_schedule())
        raw_pool = ctx.enter_context(tc.tile_pool(name="raw", bufs=RAW_BUFS))
        keep = ctx.enter_context(tc.tile_pool(name="keep", bufs=1))
        mix_pool = ctx.enter_context(tc.tile_pool(name="mix", bufs=3))
        z_pool = ctx.enter_context(tc.tile_pool(name="z", bufs=1))
        basis_pool = ctx.enter_context(tc.tile_pool(name="basis", bufs=6))
        product_pool = ctx.enter_context(tc.tile_pool(name="product", bufs=2))
        out_pool = ctx.enter_context(tc.tile_pool(name="result", bufs=3))
        sort_pool = ctx.enter_context(tc.tile_pool(name="sort", bufs=6))
        psum = ctx.enter_context(tc.psum_pool(name="psum", bufs=4))

        views = {
            "x_re": [x_re.rearrange("(g m t) k -> g m t k", g=2, t=4)[g] for g in range(2)],
            "x_im": [x_im.rearrange("(g m t) k -> g m t k", g=2, t=4)[g] for g in range(2)],
            "g_re": [g_re.rearrange("(g m t) d -> g m t d", g=2, t=4)[g] for g in range(2)],
            "g_im": [g_im.rearrange("(g m t) d -> g m t d", g=2, t=4)[g] for g in range(2)],
            "r_re": [r_re.rearrange("(p j) d -> p j d", j=PACK)],
            "r_im": [r_im.rearrange("(p j) d -> p j d", j=PACK)],
            "w": [w.rearrange("(p j) d -> p j d", j=PACK)],
            "u": [u.rearrange("(q p j) k -> q p j k", q=4, j=4)[q] for q in range(4)],
            "cos": [basis_cos.rearrange("(q p j) k -> q p j k", q=4, j=4)[m // 2][:, 2 * (m % 2) : 2 * (m % 2) + 2, :] for m in range(8)],
            "sin": [basis_sin.rearrange("(q p j) k -> q p j k", q=4, j=4)[m // 2][:, 2 * (m % 2) : 2 * (m % 2) + 2, :] for m in range(8)],
        }
        out_view = out.rearrange("(q p j) d -> q p j d", q=4, j=4)

        loads = [("x_re", 0, 0), ("x_re", 0, 1), ("r_re", 0, 0), ("x_im", 0, 0), ("x_im", 0, 1), ("r_im", 0, 0)]
        loads += [("r_re", 0, 1), ("r_im", 0, 1), ("g_re", 0, None), ("g_im", 0, None)]
        loads += [("x_re", 1, 0), ("x_re", 1, 1), ("x_im", 1, 0), ("x_im", 1, 1), ("g_re", 1, None), ("g_im", 1, None)]
        for q in range(4):
            loads += [("cos", 2 * q, None), ("sin", 2 * q, None), ("u", q, None), ("cos", 2 * q + 1, None), ("sin", 2 * q + 1, None)]
            if q == 0:
                loads += [("w", 0, None)]
        raw = {}

        def load(entries):
            for name, index, part in entries:
                src = views[name][index]
                if (name, index) not in raw:
                    raw[(name, index)] = raw_pool.tile([LANES, RAW], BF16, name="raw", align_bytes=64)
                dst = raw[(name, index)][:]
                if part is not None:
                    dst = dst[:, HALF * part : HALF * part + HALF]
                    if name in ("x_re", "x_im"):
                        src = src[:, 2 * part : 2 * part + 2, :]
                    else:
                        src = src[:, :, 256 * part : 256 * part + 256]
                nc.sync.dma_start(out=dst.rearrange("p (a b) -> p a b", a=src.shape[1]), in_=src)

        load(loads[:FIRST_LOADS])

        ident = keep.tile([LANES, LANES], F32, name="ident")
        make_identity(nc, ident[:])
        dummy = keep.tile([LANES, 1], F32, name="dummy")
        nc.vector.memset(dummy[:], 0.0)
        warm = keep.tile([LANES, 1], F32, name="warm")
        nc.scalar.activation(out=warm[:], in_=dummy[:], func=ACT.Gelu_apprx_tanh)
        ones = keep.tile([LANES, LANES], BF16, name="ones")
        nc.vector.memset(ones[:], 1.0)
        zeros = keep.tile([LANES, D], BF16, name="zeros")
        nc.vector.memset(zeros[:], 0.0)
        bias_row = keep.tile([LANES, D], BF16, name="bias_row")
        nc.vector.memset(bias_row[:], 0.0)
        nc.scalar.dma_start(out=bias_row[0:1, :], in_=bias.unsqueeze(0))
        bias_all = keep.tile([LANES, D], F32, name="bias_all")

        def quantised(columns, name):
            codes = keep.tile([LANES, columns], U32, name=name + "_codes", align_bytes=64)
            scales = keep.tile([LANES, columns], U8, name=name + "_scales", align_bytes=64)
            return codes, scales

        x_q = quantised(4 * 512, "x")
        r_q = quantised(3 * 512, "r")
        w_q = quantised(512, "w")
        z_q = quantised(4 * 512, "z")
        u_q = quantised(4 * 512, "u")
        basis_q = {}
        R_RE, R_IM, R_NEG = 0, 512, 1024

        def quantize(operand, first, columns, grouped):
            codes, scales = operand
            nc.vector.quantize_mx(
                out=codes[:, first : first + columns].bitcast(FP8X4),
                scales=scales[:, first : first + columns],
                in_=grouped,
            )

        def mx(acc, stationary, s_first, moving, m_first, columns, start, stop):
            nc.tensor.matmul_mx(
                out=acc,
                lhsT=stationary[0][:, s_first : s_first + LANES].bitcast(FP8X4),
                lhsT_scale=stationary[1][:, s_first : s_first + LANES],
                rhs=moving[0][:, m_first : m_first + columns].bitcast(FP8X4),
                rhs_scale=moving[1][:, m_first : m_first + columns],
                start=start,
                stop=stop,
            )

        to_turn = [(name, g, half) for g in range(2) for name in ("x_re", "x_im") for half in range(2)]
        for q in range(4):
            for name, index in (("cos", 2 * q), ("sin", 2 * q), ("u", q), ("cos", 2 * q + 1), ("sin", 2 * q + 1)):
                to_turn += [(name, index, half) for half in range(2)]
        to_sort = [unit for i, unit in enumerate(to_turn) if i >= SORT_FROM and i % 3 != 0]
        sorted_words = {}
        to_quantize = []

        def raw_words(name, index, half):
            return raw[(name, index)][:].bitcast(F32)[:, WORDS * half : WORDS * half + WORDS]

        def sort_ahead():
            for unit in to_turn[:SORT_AHEAD]:
                if unit in to_sort:
                    to_sort.remove(unit)
                    dst = sort_pool.tile([LANES, WORDS], F32, name="sorted", align_bytes=64)
                    nc.scalar.copy(
                        out=dst[:].rearrange("p (a e r) -> p a e r", a=2, e=2),
                        in_=raw_words(*unit).rearrange("p (a r e) -> p a e r", a=2, e=2),
                    )
                    sorted_words[unit] = dst

        def turn(count):
            for unit in to_turn[:count]:
                to_turn.remove(unit)
                words = raw_words(*unit)
                bank = psum.tile([LANES, WORDS], F32, name="turned")
                for a in range(2):
                    for e in range(2):
                        first = 256 * a + 128 * e
                        if unit in sorted_words:
                            src = sorted_words[unit][:, first : first + 128]
                        else:
                            src = words[:, 256 * a + e : 256 * a + 256 : 2]
                        nc.tensor.transpose(bank[:, first : first + 128], src, ident[:])
                nc.scalar.copy(
                    out=words.rearrange("p (a r e) -> p a r e", a=2, e=2),
                    in_=bank[:].rearrange("p (a e r) -> p a r e", a=2, e=2),
                )
                name, index, half = unit
                if half == 1:
                    to_quantize.append((name, index))

        def quantize_turned(count):
            for name, index in to_quantize[:count]:
                to_quantize.remove((name, index))
                if name in ("x_re", "x_im"):
                    operand, first = x_q, 1024 * (name == "x_im") + 512 * index
                elif name == "u":
                    operand, first = u_q, 512 * index
                else:
                    codes = basis_pool.tile([LANES, 512], U32, name="basis_codes", align_bytes=64)
                    scales = basis_pool.tile([LANES, 512], U8, name="basis_scales", align_bytes=64)
                    basis_q[(name, index)] = (codes, scales)
                    operand, first = basis_q[(name, index)], 0
                quantize(operand, first, 512, raw[(name, index)][:])

        def interleave_r(name, half):
            src = raw[(name, 0)][:, HALF * half : HALF * half + HALF].rearrange("p (j d) -> p d j", j=PACK)
            grouped = mix_pool.tile([LANES, HALF], BF16, name="r_grouped", align_bytes=64)
            dst = grouped[:].rearrange("p (d j) -> p d j", j=PACK)
            on_vector = (256 if name == "r_re" else R_IM_SPLIT) if half == 0 else 0
            if on_vector > 0:
                nc.vector.tensor_copy(out=dst[:, :on_vector, :], in_=src[:, :on_vector, :])
            if on_vector < 256:
                nc.scalar.copy(out=dst[:, on_vector:, :], in_=src[:, on_vector:, :])
            return grouped

        def negate(grouped):
            negative = mix_pool.tile([LANES, HALF], BF16, name="r_negative", bufs=2, align_bytes=64)
            nc.scalar.activation(out=negative[:], in_=grouped[:], func=ACT.Copy, scale=-1.0)
            return negative

        def quantize_r(part, half, grouped):
            quantize(r_q, part + 256 * half, 256, grouped[:])

        packed_gain = {name: keep.tile([LANES, RAW], BF16, name="packed_" + name, align_bytes=64) for name in ("g_re", "g_im")}
        w_grouped = keep.tile([LANES, RAW], BF16, name="w_grouped", align_bytes=64)
        pieces = [(packed_gain[name], (name, 1), i) for i in range(4) for name in ("g_re", "g_im")]
        pieces += [(w_grouped, ("w", 0), i) for i in range(4)]

        def by_column(tile):
            return tile[:].rearrange("p (t n) -> p n t", t=4)

        def interleaved(tile):
            return tile[:].rearrange("p (n t) -> p n t", t=4)

        def copy_piece():
            for dst, key, i in pieces[:1]:
                pieces.remove((dst, key, i))
                columns = slice(QUARTER * i, QUARTER * i + QUARTER)
                nc.scalar.copy(out=interleaved(dst)[:, columns, :], in_=by_column(raw[key])[:, columns, :])

        z_rounded = {}
        products = {}

        def mix(i, name):
            g, columns = i // 4, QUARTER * (i % 4)
            first, second = (R_IM, R_RE) if name == "y_im" else (R_RE, R_NEG)
            acc = psum.tile([LANES, WORDS], F32, name=name, tag="acc")
            for t in range(4):
                slot = acc[:, 128 * t : 128 * t + 128]
                mx(slot, x_q, 512 * g + 128 * t, r_q, first + columns, QUARTER, True, False)
                mx(slot, x_q, 1024 + 512 * g + 128 * t, r_q, second + columns, QUARTER, False, True)
            return acc

        def multiply_gains(i, y_im, y_re):
            g = i // 4
            columns = slice(QUARTER * (i % 4), QUARTER * (i % 4) + QUARTER)
            if g == 0:
                gain_re, gain_im = by_column(raw[("g_re", 0)])[:, columns, :], by_column(raw[("g_im", 0)])[:, columns, :]
            else:
                gain_re, gain_im = interleaved(packed_gain["g_re"])[:, columns, :], interleaved(packed_gain["g_im"])[:, columns, :]
            re_re = product_pool.tile([LANES, WORDS], F32, name="re_re")
            im_im = product_pool.tile([LANES, WORDS], F32, name="im_im")
            minus_re_im = product_pool.tile([LANES, WORDS], F32, name="minus_re_im")
            im_re = product_pool.tile([LANES, WORDS], F32, name="im_re")
            nc.vector.scalar_tensor_tensor(
                out=interleaved(minus_re_im), in0=by_column(y_im), scalar=-1.0, in1=gain_re, op0=ALU.mult, op1=ALU.mult
            )
            nc.vector.tensor_tensor(out=interleaved(im_im), in0=by_column(y_im), in1=gain_im, op=ALU.mult)
            nc.vector.tensor_tensor(out=interleaved(re_re), in0=by_column(y_re), in1=gain_re, op=ALU.mult)
            nc.vector.tensor_tensor(out=interleaved(im_re), in0=by_column(y_re), in1=gain_im, op=ALU.mult)
            products[i] = {"z_re": (re_re, im_im), "minus_z_im": (minus_re_im, im_re)}

        def subtract(i, engine):
            g, first = i // 4, WORDS * (i % 4)
            for name, (left, right) in products[i].items():
                if (name, g) not in z_rounded:
                    z_rounded[(name, g)] = z_pool.tile([LANES, RAW], BF16, name=name, align_bytes=64)
                engine.tensor_tensor(
                    out=z_rounded[(name, g)][:, first : first + WORDS], in0=left[:], in1=right[:], op=ALU.subtract
                )

        def quantize_z(g):
            quantize(z_q, 512 * g, 512, z_rounded[("z_re", g)][:])
            quantize(z_q, 1024 + 512 * g, 512, z_rounded[("minus_z_im", g)][:])

        turn(2)
        r_re_grouped = interleave_r("r_re", 0)
        quantize_turned(1)
        quantize_r(R_RE, 0, r_re_grouped)
        turn(2)
        idle = psum.tile([LANES, WORDS], F32, name="idle", tag="turned")
        for i in range(IDLE_MATMULS):
            nc.tensor.matmul(idle[:], lhsT=ones[:], rhs=zeros[:], start=True, stop=True)
        r_im_grouped = interleave_r("r_im", 0)
        quantize_turned(1)
        r_negative = negate(r_im_grouped)
        quantize_r(R_IM, 0, r_im_grouped)
        quantize_r(R_NEG, 0, r_negative)
        r_re_grouped = interleave_r("r_re", 1)
        r_im_grouped = interleave_r("r_im", 1)
        y_im = mix(0, "y_im")
        y_re = mix(0, "y_re")
        multiply_gains(0, y_im, y_re)
        quantize_r(R_RE, 1, r_re_grouped)
        r_negative = negate(r_im_grouped)
        quantize_r(R_IM, 1, r_im_grouped)
        quantize_r(R_NEG, 1, r_negative)

        for i in range(1, UNITS):
            y_im = mix(i, "y_im")
            turn(TURN_BETWEEN)
            sort_ahead()
            copy_piece()
            y_re = mix(i, "y_re")
            multiply_gains(i, y_im, y_re)
            if i == 1:
                subtract(0, nc.gpsimd)
            if i < UNITS - 1:
                subtract(i, nc.gpsimd)
            turn(TURN_AFTER[i])
            sort_ahead()
            if i == 4:
                quantize_z(0)
            if i == 1:
                quantize_turned(2)
            if i == UNITS - 1:
                subtract(i, nc.vector)
            copy_piece()
            if i == 1:
                load(loads[FIRST_LOADS:])
            if i == 2:
                bias_bank = psum.tile([LANES, WORDS], F32, name="bias_bank", tag="turned")
                nc.tensor.matmul(bias_bank[:], lhsT=ones[:], rhs=bias_row[:], start=True, stop=True)
                nc.scalar.copy(out=bias_all[:], in_=bias_bank[:])
        quantize(w_q, 0, 512, w_grouped[:])
        quantize_turned(3)
        quantize_z(1)

        to_finish = []

        def finish():
            for n, lo, hi, biased, result in list(to_finish):
                to_finish.remove((n, lo, hi, biased, result))
                base = D * (n % 2)
                nc.scalar.activation(out=result[:, base + lo : base + hi], in_=biased[:, lo:hi], func=ACT.Gelu_apprx_tanh)
                q, j = n // 4, n % 4
                if n >= N // LANES - 2:
                    nc.sync.dma_start(out=out_view[q][:, j, lo:hi], in_=result[:, base + lo : base + hi])
                elif n % 2 == 1:
                    nc.sync.dma_start(out=out_view[q][:, j - 1 : j + 1, :], in_=result[:].rearrange("p (a d) -> p a d", a=2))

        def quantize_for(n):
            needed = [("cos", n // 2), ("sin", n // 2), ("u", n // 4)]
            while any(key in to_quantize for key in needed):
                quantize_turned(1)

        for step in range(4):
            turn(TURN_STAGE_2)
            banks = []
            for n in range(4 * step, 4 * step + 4):
                quantize_for(n)
                for lo, hi in ((0, 256), (256, 512)) if n == N // LANES - 1 else ((0, 512),):
                    acc = psum.tile([LANES, WORDS], F32, name="field", tag="acc")
                    sums = acc[:, 0 : hi - lo]
                    mx(sums, u_q, LANES * n, w_q, lo, hi - lo, True, False)
                    for s, name in enumerate(("cos", "sin")):
                        for g in range(2):
                            mx(sums, basis_q[(name, n // 2)], 256 * (n % 2) + 128 * g, z_q, 1024 * s + 512 * g + lo, hi - lo, False, s == 1 and g == 1)
                    banks.append((n, lo, hi, sums))
            finish()
            sort_ahead()
            for n, lo, hi, sums in banks:
                if step < 3:
                    quantize_for(n + 4)
                if lo == 0:
                    biased = out_pool.tile([LANES, D], F32, name="biased")
                    if n % 2 == 0:
                        result = out_pool.tile([LANES, 2 * D], F32, name="result")
                nc.vector.tensor_tensor(out=biased[:, lo:hi], in0=sums, in1=bias_all[:, lo:hi], op=ALU.add)
                to_finish.append((n, lo, hi, biased, result))
        finish()
